import numpy as np
import ml_dtypes


def mxq(x, axis, fmt="e4m3"):
    dtype, down = {"e4m3": (ml_dtypes.float8_e4m3fn, 7), "e5m2": (ml_dtypes.float8_e5m2, 14)}[fmt]
    v = np.moveaxis(np.asarray(x, np.float32).astype(ml_dtypes.bfloat16).astype(np.float64), axis, -1)
    blocks = v.reshape(v.shape[:-1] + (-1, 32))
    amax = np.abs(blocks).max(-1, keepdims=True)
    byte = np.maximum(np.where(amax > 0, np.frexp(amax)[1] - 1 + 127, 0) - down, 1)
    scale = np.exp2(byte - 127.0)
    codes = (blocks / scale).astype(np.float32).astype(dtype).astype(np.float64)
    return np.moveaxis((codes * scale).reshape(v.shape), -1, axis)


WIDE = False


def mx_kscale(k):
    if not WIDE:
        return np.ones(k)
    levels = np.array([24, -24, 12, -12, 0])
    if k % 512:
        return np.exp2(np.random.permutation(np.resize(levels, k // 32))).repeat(32)
    a = np.empty((k // 512, 16))
    for p in range(k // 512):
        a[p, :8] = np.random.permutation(np.resize(levels, 8))
        for g in range(8):
            far = levels[np.abs(levels - a[p, g]) >= 10]
            a[p, g + 8] = far[np.random.randint(len(far))]
    return np.exp2(a.ravel()).repeat(32)


def f64(x):
    return np.asarray(x).astype(np.float64)


def striped(idx):
    return np.tile(idx.reshape(-1, 16).T, (8, 1)).astype(np.uint16)


def unstriped(offs):
    return offs[:16].T.reshape(-1).astype(np.int64)


E2M1 = np.array([0.0, 0.5, 1.0, 1.5, 2.0, 3.0, 4.0, 6.0, -0.0, -0.5, -1.0, -1.5, -2.0, -3.0, -4.0, -6.0])


def pack_weight(w, fmt):
    k, n = w.shape
    w = f64(np.asarray(w, np.float32).astype(ml_dtypes.bfloat16)).reshape(k // 32, 32, n)
    amax = np.abs(w).max(1)
    if fmt == "e4m3":
        byte = np.frexp(amax)[1] - 1 + 127 - 7
    else:
        mant, ex = np.frexp(amax / 6.0)
        byte = np.where(mant > 0.5, ex, ex - 1) + 127
    byte = np.clip(np.where(amax > 0, byte, 1), 1, 254)
    scaled = (w * np.exp2(127.0 - byte)[:, None, :]).reshape(k, n).astype(np.float32)
    by_word = np.ascontiguousarray(scaled.reshape(k // 512, 128, 4, n).transpose(0, 1, 3, 2))
    if fmt == "e4m3":
        words = by_word.astype(ml_dtypes.float8_e4m3fn).view(np.uint8)
    else:
        c = by_word.astype(ml_dtypes.float4_e2m1fn).view(np.uint8) & 0xF
        words = (c[..., 0::2] | (c[..., 1::2] << 4)).reshape(k // 512, 128, 2 * n)
    return np.ascontiguousarray(words), np.ascontiguousarray(byte.astype(np.uint8).reshape(k // 512, 16, n))


def unpack_weight(words, scales, fmt):
    g, _, n = scales.shape
    words = np.ascontiguousarray(words).reshape(g, 128, n, -1)
    if fmt == "e4m3":
        vals = words.view(ml_dtypes.float8_e4m3fn).astype(np.float64)
    else:
        nib = np.empty((g, 128, n, 4), np.uint8)
        nib[..., 0::2] = words & 0xF
        nib[..., 1::2] = words >> 4
        vals = E2M1[nib]
    vals = vals * np.repeat(np.exp2(scales.astype(np.float64) - 127.0), 8, axis=1)[..., None]
    return vals.transpose(0, 1, 3, 2).reshape(g * 512, n)


def gelu(f):
    return 0.5 * f * (1.0 + np.tanh(np.sqrt(2.0 / np.pi) * (f + 0.044715 * f**3)))


K, R, N, T, J = 1024, 512, 512, 2048, 1024


def setup_inputs():
    n = np.random.standard_normal
    s = mx_kscale(K)[:, None]
    u = mx_kscale(R)[:, None]
    p_tab = pack_weight(n((K, T)) * s, "e4m3")
    p_wu = pack_weight(n((K, R)) / np.sqrt(K) / s * u.T, "e2m1")
    return {
        "tab_words": p_tab[0],
        "tab_scales": p_tab[1],
        "wg": (n((K, R)) / np.sqrt(K) / s).astype(np.float32),
        "wu_words": p_wu[0],
        "wu_scales": p_wu[1],
        "wd": (n((R, N)) / np.sqrt(R) / u).astype(np.float32),
        "gT": (n((N, T))).astype(np.float32),
        "wgo": np.tile(np.random.uniform(0.5, 2.0, J), (128, 1)).astype(np.float32),
        "offs": striped(np.random.permutation(T)[:J]),
    }


def reference(tab_words, tab_scales, wg, wu_words, wu_scales, wd, gT, wgo, offs):
    idx = unstriped(offs)
    tab_ = unpack_weight(tab_words, tab_scales, "e4m3")[:, idx]
    wg_ = mxq(f64(wg), 0, "e4m3")
    wu_ = unpack_weight(wu_words, wu_scales, "e2m1")
    ga = wg_.T @ tab_
    ub = wu_.T @ tab_
    h = gelu(ga) * ub
    h_ = mxq(h, 0, "e4m3")
    wd_ = mxq(f64(wd), 0, "e4m3")
    y = wd_.T @ h_
    out = np.zeros((N, T))
    out[:, idx] = f64(wgo)[0] * (y * f64(gT)[:, idx])
    return out

@@ -1,0 +1,238 @@
+from contextlib import ExitStack
+
+import concourse.mybir as mybir
+
+K, R, N, T, J = 1024, 512, 512, 2048, 1024
+FLOPS = 2 * J * (2 * K * R + R * N)
+
+F32 = mybir.dt.float32
+BF16 = mybir.dt.bfloat16
+I32 = mybir.dt.int32
+U32 = mybir.dt.uint32
+U16 = mybir.dt.uint16
+U8 = mybir.dt.uint8
+FP8X4 = mybir.dt.float8_e4m3fn_x4
+FP4X4 = mybir.dt.float4_e2m1fn_x4
+MULT = mybir.AluOpType.mult
+GELU = mybir.ActivationFunctionType.Gelu_apprx_tanh
+
+P = 128
+PACK = 4
+K_PASS = P * PACK
+PASSES = K // K_PASS
+QUADS = 4
+HALF = J // 2
+J_TILES = J // P
+N_TILES = N // P
+PAGES = N_TILES
+
+
+def tile_list_modp_ggelu_gate_kernel(
+    tc, tab_words, tab_scales, wg, wu_words, wu_scales, wd, gT, wgo, offs, out
+):
+    nc = tc.nc
+    with ExitStack() as ctx:
+        keep = ctx.enter_context(tc.tile_pool(name="keep", bufs=1))
+        ring = ctx.enter_context(tc.tile_pool(name="ring", bufs=2))
+        psum = ctx.enter_context(tc.psum_pool(name="psum", bufs=2))
+
+        def held(name, shape, dtype):
+            return keep.tile(shape, dtype, name=name, tag=name, align_bytes=64)
+
+        offsets = keep.tile([P, J // 16], U16, name="offsets")
+        nc.sync.dma_start(offsets[:], offs)
+
+        tab_plane = held("tab_plane", [P, T], U8)
+        wu_plane_raw = held("wu_plane_raw", [P, PASSES * R], U8)
+        tok_plane1 = held("tok_plane1", [P, J], U8)
+        nc.vector.memset(tab_plane[:].bitcast(I32), 0)
+        nc.vector.memset(wu_plane_raw[:].bitcast(I32), 0)
+        nc.vector.memset(tok_plane1[:].bitcast(I32), 0)
+        warm = held("warm", [P, 1], F32)
+        warm2 = held("warm2", [P, 1], F32)
+        nc.gpsimd.memset(warm[:], 0.0)
+        pages = [held("page%d" % i, [P, T], F32) for i in range(PAGES)]
+        for page in pages:
+            nc.gpsimd.memset(page[:], 0.0)
+
+        tab = [held("tab%d" % a, [P, T], I32) for a in range(PASSES)]
+        gates = [held("gates%d" % n, [P, T], F32) for n in range(N_TILES)]
+        wg_raw = [held("wg_raw%d" % a, [P, PACK, R], F32) for a in range(PASSES)]
+        wu_raw = held("wu_raw", [P, PASSES, R // 2], I32)
+        wd_raw = held("wd_raw", [P, PACK, N], F32)
+        router = held("router", [P, J], F32)
+
+        for q in range(QUADS):
+            nc.scalar.dma_start(
+                tab_plane[32 * q : 32 * q + 8, :].bitcast(I32),
+                tab_scales[:, 4 * q : 4 * q + 4, :].bitcast(I32),
+            )
+        for q in range(QUADS):
+            nc.scalar.dma_start(
+                wu_plane_raw[32 * q : 32 * q + 4, :].bitcast(I32).rearrange("p (a w) -> p a w", a=PASSES),
+                wu_scales[:, 4 * q : 4 * q + 4, :].bitcast(I32).rearrange("a p w -> p a w"),
+            )
+        nc.scalar.activation(warm2[:], warm[:], GELU)
+
+        def load_gates(n):
+            nc.sync.dma_start(gates[n][:], gT[P * n : P * (n + 1), :])
+
+        def load_wg(a):
+            nc.sync.dma_start(
+                wg_raw[a][:], wg[K_PASS * a : K_PASS * (a + 1), :].rearrange("(p i) r -> p i r", i=PACK)
+            )
+
+        for a in range(PASSES):
+            nc.sync.dma_start(tab[a][:], tab_words[a].rearrange("p t i -> p (t i)").bitcast(I32))
+            load_wg(a)
+        nc.sync.dma_start(wu_raw[:], wu_words.bitcast(I32).rearrange("a p w -> p a w"))
+        nc.sync.dma_start(router[:], wgo)
+        load_gates(0)
+        load_gates(1)
+        wd_rows = wd.rearrange("(g s q) n -> s g q n", s=PACK, q=8)
+        for s in range(PACK):
+            nc.sync.dma_start(wd_raw[:, s, :], wd_rows[s])
+        load_gates(2)
+        load_gates(3)
+
+        tok = [held("tok%d" % a, [P, J], U32) for a in range(PASSES)]
+        tok_plane = held("tok_plane", [P, J], U8)
+        nc.vector.tensor_copy(tok[0][:], tab[0][:].bitcast(U32).indirect(offsets[:]))
+        nc.vector.tensor_copy(tok_plane[:], tab_plane[:].indirect(offsets[:]))
+        nc.vector.tensor_copy(tok[1][:], tab[1][:].bitcast(U32).indirect(offsets[:]))
+        for q in range(QUADS):
+            nc.scalar.dma_start(
+                tok_plane1[32 * q : 32 * q + 4, :].bitcast(I32),
+                tok_plane[32 * q + 4 : 32 * q + 8, :].bitcast(I32),
+            )
+
+        gated = {}
+
+        def gather_gates(n, tag):
+            gated[n] = keep.tile([P, J], F32, name="gated%d" % n, tag=tag, align_bytes=64)
+            nc.vector.tensor_tensor(gated[n][:], gates[n][:].indirect(offsets[:]), router[:], MULT)
+
+        wu = held("wu", [P, PASSES, 2 * R], U8)
+        wu_plane = held("wu_plane", [P, PASSES, R], U8)
+        for a in range(PASSES):
+            nc.vector.tensor_copy(
+                wu[:, a, :].bitcast(I32).rearrange("p (s g w) -> p s g w", s=PACK, w=4),
+                wu_raw[:, a, :].rearrange("p (g s w) -> p s g w", s=PACK, w=4),
+            )
+            nc.vector.tensor_copy(
+                wu_plane[:, a, :].bitcast(I32).rearrange("p (s g w) -> p s g w", s=PACK, w=2),
+                wu_plane_raw[:, R * a : R * (a + 1)].bitcast(I32).rearrange("p (g s w) -> p s g w", s=PACK, w=2),
+            )
+
+        wg_codes = [held("wg_codes%d" % a, [P, R], U32) for a in range(PASSES)]
+        wg_plane = [held("wg_plane%d" % a, [P, R], U8) for a in range(PASSES)]
+        for a in range(PASSES):
+            wg_bf = held("wg_bf%d" % a, [P, PACK * R], BF16)
+            dst = wg_bf[:].rearrange("p (s g u c i) -> p s g u i c", s=PACK, u=2, c=4, i=PACK)
+            src = wg_raw[a][:].rearrange("p i (g s u c) -> p s g u i c", s=PACK, u=2, c=4)
+            for s in range(PACK):
+                nc.scalar.copy(dst[:, s], src[:, s])
+                if s % 2 == 1:
+                    cols = slice(P * (s - 1), P * (s + 1))
+                    nc.vector.quantize_mx(
+                        out=wg_codes[a][:, cols].bitcast(FP8X4),
+                        scales=wg_plane[a][:, cols],
+                        in_=wg_bf[:, K_PASS * (s - 1) : K_PASS * (s + 1)],
+                    )
+
+        gather_gates(0, "gated0")
+
+        wd_codes = held("wd_codes", [P, N], U32)
+        wd_plane = held("wd_plane", [P, N], U8)
+        wd_bf = held("wd_bf", [P, PACK * N], BF16)
+
+        def quantise_wd():
+            dst = wd_bf[:].rearrange("p (u m c s) -> p u m s c", u=2, c=4, s=PACK)
+            src = wd_raw[:].rearrange("p s (u m c) -> p u m s c", u=2, c=4)
+            for u in range(2):
+                nc.scalar.copy(dst[:, u], src[:, u])
+            nc.vector.quantize_mx(out=wd_codes[:].bitcast(FP8X4), scales=wd_plane[:], in_=wd_bf[:])
+
+        h_bf = [held("h_bf%d" % u, [P, HALF * PACK], BF16) for u in range(2)]
+        h_codes = [held("h_codes%d" % u, [P, HALF], U32) for u in range(2)]
+        h_plane = [held("h_plane%d" % u, [P, HALF], U8) for u in range(2)]
+        y = [held("y%d" % u, [P, N_TILES, HALF], F32) for u in range(2)]
+
+        def first_stage(jt):
+            cols = slice(P * jt, P * (jt + 1))
+            ga = psum.tile([P, PACK, P], F32, name="ga", bufs=3)
+            ub = psum.tile([P, PACK, P], F32, name="ub", bufs=3)
+            for s in range(PACK):
+                for a in range(PASSES):
+                    nc.tensor.matmul_mx(
+                        out=ga[:, s, :],
+                        lhsT=wg_codes[a][:, P * s : P * (s + 1)].bitcast(FP8X4),
+                        lhsT_scale=wg_plane[a][:, P * s : P * (s + 1)],
+                        rhs=tok[a][:, cols].bitcast(FP8X4),
+                        rhs_scale=tok_plane[4 * a : P, cols],
+                        start=(a == 0),
+                        stop=(a == PASSES - 1),
+                    )
+            for s in range(PACK):
+                for a in range(PASSES):
+                    nc.tensor.matmul_mx(
+                        out=ub[:, s, :],
+                        lhsT=wu[:, a, 2 * P * s : 2 * P * (s + 1)].bitcast(FP4X4),
+                        lhsT_scale=wu_plane[:, a, P * s : P * (s + 1)],
+                        rhs=tok[a][:, cols].bitcast(FP8X4),
+                        rhs_scale=(tok_plane, tok_plane1)[a][:, cols],
+                        start=(a == 0),
+                        stop=(a == PASSES - 1),
+                    )
+            act = ring.tile([P, P, PACK], F32, name="act", bufs=3)
+            nc.scalar.activation(act[:], ga[:].rearrange("p s j -> p j s"), GELU)
+            u, place = divmod(jt, J_TILES // 2)
+            nc.vector.tensor_tensor(
+                h_bf[u][:, K_PASS * place : K_PASS * (place + 1)].rearrange("p (j s) -> p j s", s=PACK),
+                ub[:].rearrange("p s j -> p j s"),
+                act[:],
+                MULT,
+            )
+
+        def second_stage(u):
+            nc.vector.quantize_mx(out=h_codes[u][:].bitcast(FP8X4), scales=h_plane[u][:], in_=h_bf[u][:])
+            for n in range(N_TILES):
+                acc = psum.tile([P, HALF], F32, name="acc")
+                nc.tensor.matmul_mx(
+                    out=acc[:],
+                    lhsT=wd_codes[:, P * n : P * (n + 1)].bitcast(FP8X4),
+                    lhsT_scale=wd_plane[:, P * n : P * (n + 1)],
+                    rhs=h_codes[u][:].bitcast(FP8X4),
+                    rhs_scale=h_plane[u][:],
+                    start=True,
+                    stop=True,
+                )
+                nc.scalar.copy(y[u][:, n, :], acc[:])
+
+        def scatter(n, u):
+            nc.vector.tensor_tensor(
+                pages[n % PAGES][:].indirect(offsets[:, (HALF // 16) * u : (HALF // 16) * (u + 1)]),
+                y[u][:, n, :],
+                gated[n][:, HALF * u : HALF * (u + 1)],
+                MULT,
+            )
+
+        def store(n):
+            nc.sync.dma_start(out[P * n : P * (n + 1), :], pages[n % PAGES][:])
+
+        for jt in range(J_TILES // 2):
+            first_stage(jt)
+            if jt == 1:
+                gather_gates(1, "gated1")
+        quantise_wd()
+        second_stage(0)
+        gather_gates(2, "gated2")
+        for jt in range(J_TILES // 2, J_TILES):
+            first_stage(jt)
+        second_stage(1)
+        gather_gates(3, "h_bf1")
+        for u in range(2):
+            for n in range(N_TILES):
+                scatter(n, u)
+                if u == 1:
+                    store(n)

@@ -24,7 +24,7 @@ QUADS = 4
 HALF = J // 2
 J_TILES = J // P
 N_TILES = N // P
-PAGES = N_TILES
+PAGES = 3
 
 
 def tile_list_modp_ggelu_gate_kernel(
@@ -42,37 +42,31 @@ def tile_list_modp_ggelu_gate_kernel(
         offsets = keep.tile([P, J // 16], U16, name="offsets")
         nc.sync.dma_start(offsets[:], offs)
 
-        tab_plane = held("tab_plane", [P, T], U8)
-        wu_plane_raw = held("wu_plane_raw", [P, PASSES * R], U8)
-        tok_plane1 = held("tok_plane1", [P, J], U8)
-        nc.vector.memset(tab_plane[:].bitcast(I32), 0)
-        nc.vector.memset(wu_plane_raw[:].bitcast(I32), 0)
-        nc.vector.memset(tok_plane1[:].bitcast(I32), 0)
+        tab_rows = held("tab_rows", [P, T], U8)
+        tok_planes = held("tok_planes", [P, PASSES * J], U8)
+        wu_planes = held("wu_planes", [P, PASSES * R], U8)
+        nc.vector.memset(tab_rows[32:64, :].bitcast(I32), 0)
+        nc.vector.memset(tab_rows[64:128, :].bitcast(I32), 0)
+        nc.vector.memset(tok_planes[:].bitcast(I32), 0)
+        nc.vector.memset(wu_planes[:].bitcast(I32), 0)
         warm = held("warm", [P, 1], F32)
         warm2 = held("warm2", [P, 1], F32)
         nc.gpsimd.memset(warm[:], 0.0)
-        pages = [held("page%d" % i, [P, T], F32) for i in range(PAGES)]
+        nc.scalar.activation(warm2[:], warm[:], GELU)
+        pages = [held("page%d" % i, [P, T], F32) for i in range(PAGES - 1)]
         for page in pages:
-            nc.gpsimd.memset(page[:], 0.0)
+            nc.vector.memset(page[:], 0.0)
 
         tab = [held("tab%d" % a, [P, T], I32) for a in range(PASSES)]
         gates = [held("gates%d" % n, [P, T], F32) for n in range(N_TILES)]
         wg_raw = [held("wg_raw%d" % a, [P, PACK, R], F32) for a in range(PASSES)]
         wu_raw = held("wu_raw", [P, PASSES, R // 2], I32)
+        wu_rows_raw = held("wu_rows_raw", [32, R // 4], I32)
         wd_raw = held("wd_raw", [P, PACK, N], F32)
         router = held("router", [P, J], F32)
 
-        for q in range(QUADS):
-            nc.scalar.dma_start(
-                tab_plane[32 * q : 32 * q + 8, :].bitcast(I32),
-                tab_scales[:, 4 * q : 4 * q + 4, :].bitcast(I32),
-            )
-        for q in range(QUADS):
-            nc.scalar.dma_start(
-                wu_plane_raw[32 * q : 32 * q + 4, :].bitcast(I32).rearrange("p (a w) -> p a w", a=PASSES),
-                wu_scales[:, 4 * q : 4 * q + 4, :].bitcast(I32).rearrange("a p w -> p a w"),
-            )
-        nc.scalar.activation(warm2[:], warm[:], GELU)
+        def load_tab(a):
+            nc.sync.dma_start(tab[a][:], tab_words[a].rearrange("p t i -> p (t i)").bitcast(I32))
 
         def load_gates(n):
             nc.sync.dma_start(gates[n][:], gT[P * n : P * (n + 1), :])
@@ -82,10 +76,13 @@ def tile_list_modp_ggelu_gate_kernel(
                 wg_raw[a][:], wg[K_PASS * a : K_PASS * (a + 1), :].rearrange("(p i) r -> p i r", i=PACK)
             )
 
-        for a in range(PASSES):
-            nc.sync.dma_start(tab[a][:], tab_words[a].rearrange("p t i -> p (t i)").bitcast(I32))
-            load_wg(a)
+        nc.sync.dma_start(tab_rows[0:32, :].bitcast(I32), tab_scales.bitcast(I32).rearrange("a b w -> b a w"))
+        load_tab(0)
+        load_wg(0)
+        nc.sync.dma_start(wu_rows_raw[:], wu_scales.bitcast(I32).rearrange("a b w -> b a w"))
         nc.sync.dma_start(wu_raw[:], wu_words.bitcast(I32).rearrange("a p w -> p a w"))
+        load_tab(1)
+        load_wg(1)
         nc.sync.dma_start(router[:], wgo)
         load_gates(0)
         load_gates(1)
@@ -95,16 +92,18 @@ def tile_list_modp_ggelu_gate_kernel(
         load_gates(2)
         load_gates(3)
 
+        def spread_rows(planes, rows):
+            for q in range(QUADS):
+                nc.scalar.dma_start(planes[32 * q : 32 * q + 4, :].bitcast(I32), rows[8 * q : 8 * q + 8, :])
+
         tok = [held("tok%d" % a, [P, J], U32) for a in range(PASSES)]
-        tok_plane = held("tok_plane", [P, J], U8)
-        nc.vector.tensor_copy(tok[0][:], tab[0][:].bitcast(U32).indirect(offsets[:]))
-        nc.vector.tensor_copy(tok_plane[:], tab_plane[:].indirect(offsets[:]))
-        nc.vector.tensor_copy(tok[1][:], tab[1][:].bitcast(U32).indirect(offsets[:]))
-        for q in range(QUADS):
-            nc.scalar.dma_start(
-                tok_plane1[32 * q : 32 * q + 4, :].bitcast(I32),
-                tok_plane[32 * q + 4 : 32 * q + 8, :].bitcast(I32),
-            )
+        tok_rows = held("tok_rows", [P, J], U8)
+        nc.vector.tensor_copy(tok_rows[:], tab_rows[:].indirect(offsets[:]))
+        spread_rows(tok_planes, tok_rows[:].bitcast(I32))
+        for a in range(PASSES):
+            nc.vector.tensor_copy(tok[a][:], tab[a][:].bitcast(U32).indirect(offsets[:]))
+        pages.append(keep.tile([P, T], F32, name="page2", tag="tab1", align_bytes=64))
+        nc.vector.memset(pages[-1][:], 0.0)
 
         gated = {}
 
@@ -113,15 +112,16 @@ def tile_list_modp_ggelu_gate_kernel(
             nc.vector.tensor_tensor(gated[n][:], gates[n][:].indirect(offsets[:]), router[:], MULT)
 
         wu = held("wu", [P, PASSES, 2 * R], U8)
-        wu_plane = held("wu_plane", [P, PASSES, R], U8)
+        wu_rows = held("wu_rows", [32, R // 4], I32)
+        nc.vector.tensor_copy(
+            wu_rows[:].rearrange("p (s g w) -> p s g w", s=PACK, w=2),
+            wu_rows_raw[:].rearrange("p (g s w) -> p s g w", s=PACK, w=2),
+        )
+        spread_rows(wu_planes, wu_rows[:])
         for a in range(PASSES):
             nc.vector.tensor_copy(
                 wu[:, a, :].bitcast(I32).rearrange("p (s g w) -> p s g w", s=PACK, w=4),
                 wu_raw[:, a, :].rearrange("p (g s w) -> p s g w", s=PACK, w=4),
-            )
-            nc.vector.tensor_copy(
-                wu_plane[:, a, :].bitcast(I32).rearrange("p (s g w) -> p s g w", s=PACK, w=2),
-                wu_plane_raw[:, R * a : R * (a + 1)].bitcast(I32).rearrange("p (g s w) -> p s g w", s=PACK, w=2),
             )
 
         wg_codes = [held("wg_codes%d" % a, [P, R], U32) for a in range(PASSES)]
@@ -160,8 +160,8 @@ def tile_list_modp_ggelu_gate_kernel(
 
         def first_stage(jt):
             cols = slice(P * jt, P * (jt + 1))
-            ga = psum.tile([P, PACK, P], F32, name="ga", bufs=3)
-            ub = psum.tile([P, PACK, P], F32, name="ub", bufs=3)
+            ga = psum.tile([P, PACK, P], F32, name="ga", bufs=2)
+            ub = psum.tile([P, PACK, P], F32, name="ub", bufs=5)
             for s in range(PACK):
                 for a in range(PASSES):
                     nc.tensor.matmul_mx(
@@ -169,7 +169,7 @@ def tile_list_modp_ggelu_gate_kernel(
                         lhsT=wg_codes[a][:, P * s : P * (s + 1)].bitcast(FP8X4),
                         lhsT_scale=wg_plane[a][:, P * s : P * (s + 1)],
                         rhs=tok[a][:, cols].bitcast(FP8X4),
-                        rhs_scale=tok_plane[4 * a : P, cols],
+                        rhs_scale=tok_planes[:, J * a + P * jt : J * a + P * (jt + 1)],
                         start=(a == 0),
                         stop=(a == PASSES - 1),
                     )
@@ -178,9 +178,9 @@ def tile_list_modp_ggelu_gate_kernel(
                     nc.tensor.matmul_mx(
                         out=ub[:, s, :],
                         lhsT=wu[:, a, 2 * P * s : 2 * P * (s + 1)].bitcast(FP4X4),
-                        lhsT_scale=wu_plane[:, a, P * s : P * (s + 1)],
+                        lhsT_scale=wu_planes[:, R * a + P * s : R * a + P * (s + 1)],
                         rhs=tok[a][:, cols].bitcast(FP8X4),
-                        rhs_scale=(tok_plane, tok_plane1)[a][:, cols],
+                        rhs_scale=tok_planes[:, J * a + P * jt : J * a + P * (jt + 1)],
                         start=(a == 0),
                         stop=(a == PASSES - 1),
                     )
@@ -197,7 +197,7 @@ def tile_list_modp_ggelu_gate_kernel(
         def second_stage(u):
             nc.vector.quantize_mx(out=h_codes[u][:].bitcast(FP8X4), scales=h_plane[u][:], in_=h_bf[u][:])
             for n in range(N_TILES):
-                acc = psum.tile([P, HALF], F32, name="acc")
+                acc = psum.tile([P, HALF], F32, name="acc", bufs=1)
                 nc.tensor.matmul_mx(
                     out=acc[:],
                     lhsT=wd_codes[:, P * n : P * (n + 1)].bitcast(FP8X4),
@@ -232,7 +232,11 @@ def tile_list_modp_ggelu_gate_kernel(
         second_stage(1)
         gather_gates(3, "h_bf1")
         for u in range(2):
-            for n in range(N_TILES):
+            for n in range(PAGES):
                 scatter(n, u)
                 if u == 1:
                     store(n)
+        for n in range(PAGES, N_TILES):
+            for u in range(2):
+                scatter(n, u)
+            store(n)

@@ -25,6 +25,7 @@ HALF = J // 2
 J_TILES = J // P
 N_TILES = N // P
 PAGES = 3
+UP_BANKS = 5
 
 
 def tile_list_modp_ggelu_gate_kernel(
@@ -36,8 +37,8 @@ def tile_list_modp_ggelu_gate_kernel(
         ring = ctx.enter_context(tc.tile_pool(name="ring", bufs=2))
         psum = ctx.enter_context(tc.psum_pool(name="psum", bufs=2))
 
-        def held(name, shape, dtype):
-            return keep.tile(shape, dtype, name=name, tag=name, align_bytes=64)
+        def held(name, shape, dtype, after=None):
+            return keep.tile(shape, dtype, name=name, tag=after or name, align_bytes=64)
 
         offsets = keep.tile([P, J // 16], U16, name="offsets")
         nc.sync.dma_start(offsets[:], offs)
@@ -54,21 +55,19 @@ def tile_list_modp_ggelu_gate_kernel(
         nc.gpsimd.memset(warm[:], 0.0)
         nc.scalar.activation(warm2[:], warm[:], GELU)
         pages = [held("page%d" % i, [P, T], F32) for i in range(PAGES - 1)]
-        for page in pages:
-            nc.vector.memset(page[:], 0.0)
 
         tab = [held("tab%d" % a, [P, T], I32) for a in range(PASSES)]
-        gates = [held("gates%d" % n, [P, T], F32) for n in range(N_TILES)]
+        gates = {}
         wg_raw = [held("wg_raw%d" % a, [P, PACK, R], F32) for a in range(PASSES)]
         wu_raw = held("wu_raw", [P, PASSES, R // 2], I32)
         wu_rows_raw = held("wu_rows_raw", [32, R // 4], I32)
-        wd_raw = held("wd_raw", [P, PACK, N], F32)
         router = held("router", [P, J], F32)
 
         def load_tab(a):
             nc.sync.dma_start(tab[a][:], tab_words[a].rearrange("p t i -> p (t i)").bitcast(I32))
 
-        def load_gates(n):
+        def load_gates(n, after=None):
+            gates[n] = held("gates%d" % n, [P, T], F32, after)
             nc.sync.dma_start(gates[n][:], gT[P * n : P * (n + 1), :])
 
         def load_wg(a):
@@ -77,33 +76,35 @@ def tile_list_modp_ggelu_gate_kernel(
             )
 
         nc.sync.dma_start(tab_rows[0:32, :].bitcast(I32), tab_scales.bitcast(I32).rearrange("a b w -> b a w"))
+        nc.sync.dma_start(wu_rows_raw[:], wu_scales.bitcast(I32).rearrange("a b w -> b a w"))
         load_tab(0)
         load_wg(0)
-        nc.sync.dma_start(wu_rows_raw[:], wu_scales.bitcast(I32).rearrange("a b w -> b a w"))
         nc.sync.dma_start(wu_raw[:], wu_words.bitcast(I32).rearrange("a p w -> p a w"))
         load_tab(1)
         load_wg(1)
         nc.sync.dma_start(router[:], wgo)
         load_gates(0)
-        load_gates(1)
-        wd_rows = wd.rearrange("(g s q) n -> s g q n", s=PACK, q=8)
-        for s in range(PACK):
-            nc.sync.dma_start(wd_raw[:, s, :], wd_rows[s])
-        load_gates(2)
-        load_gates(3)
 
-        def spread_rows(planes, rows):
+        def spread_rows(queue, planes, rows):
             for q in range(QUADS):
-                nc.scalar.dma_start(planes[32 * q : 32 * q + 4, :].bitcast(I32), rows[8 * q : 8 * q + 8, :])
+                queue.dma_start(planes[32 * q : 32 * q + 4, :].bitcast(I32), rows[8 * q : 8 * q + 8, :])
+
+        wu_rows = held("wu_rows", [32, R // 4], I32)
+        nc.vector.tensor_copy(
+            wu_rows[:].rearrange("p (s g w) -> p s g w", s=PACK, w=2),
+            wu_rows_raw[:].rearrange("p (g s w) -> p s g w", s=PACK, w=2),
+        )
+        spread_rows(nc.scalar, wu_planes, wu_rows[:])
 
         tok = [held("tok%d" % a, [P, J], U32) for a in range(PASSES)]
         tok_rows = held("tok_rows", [P, J], U8)
         nc.vector.tensor_copy(tok_rows[:], tab_rows[:].indirect(offsets[:]))
-        spread_rows(tok_planes, tok_rows[:].bitcast(I32))
+        spread_rows(nc.gpsimd, tok_planes, tok_rows[:].bitcast(I32))
         for a in range(PASSES):
             nc.vector.tensor_copy(tok[a][:], tab[a][:].bitcast(U32).indirect(offsets[:]))
-        pages.append(keep.tile([P, T], F32, name="page2", tag="tab1", align_bytes=64))
-        nc.vector.memset(pages[-1][:], 0.0)
+        pages.append(held("page2", [P, T], F32, after="tab0"))
+        for page in pages:
+            nc.vector.memset(page[:], 0.0)
 
         gated = {}
 
@@ -112,12 +113,6 @@ def tile_list_modp_ggelu_gate_kernel(
             nc.vector.tensor_tensor(gated[n][:], gates[n][:].indirect(offsets[:]), router[:], MULT)
 
         wu = held("wu", [P, PASSES, 2 * R], U8)
-        wu_rows = held("wu_rows", [32, R // 4], I32)
-        nc.vector.tensor_copy(
-            wu_rows[:].rearrange("p (s g w) -> p s g w", s=PACK, w=2),
-            wu_rows_raw[:].rearrange("p (g s w) -> p s g w", s=PACK, w=2),
-        )
-        spread_rows(wu_planes, wu_rows[:])
         for a in range(PASSES):
             nc.vector.tensor_copy(
                 wu[:, a, :].bitcast(I32).rearrange("p (s g w) -> p s g w", s=PACK, w=4),
@@ -140,7 +135,15 @@ def tile_list_modp_ggelu_gate_kernel(
                         in_=wg_bf[:, K_PASS * (s - 1) : K_PASS * (s + 1)],
                     )
 
+        load_gates(1, after="wg_raw0")
+        wd_raw = held("wd_raw", [P, PACK, N], F32, after="tab1")
+        wd_rows = wd.rearrange("(g s q) n -> s g q n", s=PACK, q=8)
+        for s in range(PACK):
+            nc.sync.dma_start(wd_raw[:, s, :], wd_rows[s])
+        load_gates(2, after="wg_raw1")
         gather_gates(0, "gated0")
+        load_gates(3, after="gates0")
+        gather_gates(1, "gated1")
 
         wd_codes = held("wd_codes", [P, N], U32)
         wd_plane = held("wd_plane", [P, N], U8)
@@ -158,41 +161,49 @@ def tile_list_modp_ggelu_gate_kernel(
         h_plane = [held("h_plane%d" % u, [P, HALF], U8) for u in range(2)]
         y = [held("y%d" % u, [P, N_TILES, HALF], F32) for u in range(2)]
 
+        ups = {}
+
+        def first_product(acc, jt, weights, planes):
+            for s in range(PACK):
+                for a in range(PASSES):
+                    nc.tensor.matmul_mx(
+                        out=acc[:, s, :],
+                        lhsT=weights(a, s),
+                        lhsT_scale=planes(a, s),
+                        rhs=tok[a][:, P * jt : P * (jt + 1)].bitcast(FP8X4),
+                        rhs_scale=tok_planes[:, J * a + P * jt : J * a + P * (jt + 1)],
+                        start=(a == 0),
+                        stop=(a == PASSES - 1),
+                    )
+
+        def up_product(jt):
+            ups[jt] = psum.tile([P, PACK, P], F32, name="ub", bufs=UP_BANKS)
+            first_product(
+                ups[jt],
+                jt,
+                lambda a, s: wu[:, a, 2 * P * s : 2 * P * (s + 1)].bitcast(FP4X4),
+                lambda a, s: wu_planes[:, R * a + P * s : R * a + P * (s + 1)],
+            )
+
         def first_stage(jt):
-            cols = slice(P * jt, P * (jt + 1))
             ga = psum.tile([P, PACK, P], F32, name="ga", bufs=2)
-            ub = psum.tile([P, PACK, P], F32, name="ub", bufs=5)
-            for s in range(PACK):
-                for a in range(PASSES):
-                    nc.tensor.matmul_mx(
-                        out=ga[:, s, :],
-                        lhsT=wg_codes[a][:, P * s : P * (s + 1)].bitcast(FP8X4),
-                        lhsT_scale=wg_plane[a][:, P * s : P * (s + 1)],
-                        rhs=tok[a][:, cols].bitcast(FP8X4),
-                        rhs_scale=tok_planes[:, J * a + P * jt : J * a + P * (jt + 1)],
-                        start=(a == 0),
-                        stop=(a == PASSES - 1),
-                    )
-            for s in range(PACK):
-                for a in range(PASSES):
-                    nc.tensor.matmul_mx(
-                        out=ub[:, s, :],
-                        lhsT=wu[:, a, 2 * P * s : 2 * P * (s + 1)].bitcast(FP4X4),
-                        lhsT_scale=wu_planes[:, R * a + P * s : R * a + P * (s + 1)],
-                        rhs=tok[a][:, cols].bitcast(FP8X4),
-                        rhs_scale=tok_planes[:, J * a + P * jt : J * a + P * (jt + 1)],
-                        start=(a == 0),
-                        stop=(a == PASSES - 1),
-                    )
+            first_product(
+                ga,
+                jt,
+                lambda a, s: wg_codes[a][:, P * s : P * (s + 1)].bitcast(FP8X4),
+                lambda a, s: wg_plane[a][:, P * s : P * (s + 1)],
+            )
             act = ring.tile([P, P, PACK], F32, name="act", bufs=3)
             nc.scalar.activation(act[:], ga[:].rearrange("p s j -> p j s"), GELU)
             u, place = divmod(jt, J_TILES // 2)
             nc.vector.tensor_tensor(
                 h_bf[u][:, K_PASS * place : K_PASS * (place + 1)].rearrange("p (j s) -> p j s", s=PACK),
-                ub[:].rearrange("p s j -> p j s"),
+                ups[jt][:].rearrange("p s j -> p j s"),
                 act[:],
                 MULT,
             )
+            if jt + UP_BANKS < J_TILES:
+                up_product(jt + UP_BANKS)
 
         def second_stage(u):
             nc.vector.quantize_mx(out=h_codes[u][:].bitcast(FP8X4), scales=h_plane[u][:], in_=h_bf[u][:])
@@ -220,10 +231,10 @@ def tile_list_modp_ggelu_gate_kernel(
         def store(n):
             nc.sync.dma_start(out[P * n : P * (n + 1), :], pages[n % PAGES][:])
 
+        for jt in range(UP_BANKS):
+            up_product(jt)
         for jt in range(J_TILES // 2):
             first_stage(jt)
-            if jt == 1:
-                gather_gates(1, "gated1")
         quantise_wd()
         second_stage(0)
         gather_gates(2, "gated2")

@@ -53,56 +53,58 @@ def tile_list_modp_ggelu_gate_kernel(
         warm = held("warm", [P, 1], F32)
         warm2 = held("warm2", [P, 1], F32)
         nc.gpsimd.memset(warm[:], 0.0)
-        nc.scalar.activation(warm2[:], warm[:], GELU)
         pages = [held("page%d" % i, [P, T], F32) for i in range(PAGES - 1)]
 
         tab = [held("tab%d" % a, [P, T], I32) for a in range(PASSES)]
         gates = {}
-        wg_raw = [held("wg_raw%d" % a, [P, PACK, R], F32) for a in range(PASSES)]
+        wg_raw = {}
         wu_raw = held("wu_raw", [P, PASSES, R // 2], I32)
-        wu_rows_raw = held("wu_rows_raw", [32, R // 4], I32)
-        router = held("router", [P, J], F32)
+        wu_planes_raw = held("wu_planes_raw", [P, PASSES, R // 4], I32)
 
         def load_tab(a):
             nc.sync.dma_start(tab[a][:], tab_words[a].rearrange("p t i -> p (t i)").bitcast(I32))
 
-        def load_gates(n, after=None):
+        def load_gates(n, after):
             gates[n] = held("gates%d" % n, [P, T], F32, after)
             nc.sync.dma_start(gates[n][:], gT[P * n : P * (n + 1), :])
 
-        def load_wg(a):
+        def load_wg(a, after):
+            wg_raw[a] = held("wg_raw%d" % a, [P, PACK, R], F32, after)
             nc.sync.dma_start(
                 wg_raw[a][:], wg[K_PASS * a : K_PASS * (a + 1), :].rearrange("(p i) r -> p i r", i=PACK)
             )
 
         nc.sync.dma_start(tab_rows[0:32, :].bitcast(I32), tab_scales.bitcast(I32).rearrange("a b w -> b a w"))
-        nc.sync.dma_start(wu_rows_raw[:], wu_scales.bitcast(I32).rearrange("a b w -> b a w"))
+        for q in range(QUADS):
+            nc.scalar.dma_start(
+                wu_planes_raw[32 * q : 32 * q + 4],
+                wu_scales[:, 4 * q : 4 * q + 4, :].bitcast(I32).rearrange("a p w -> p a w"),
+            )
+        nc.scalar.activation(warm2[:], warm[:], GELU)
         load_tab(0)
-        load_wg(0)
+        load_wg(0, "wg_raw0")
         nc.sync.dma_start(wu_raw[:], wu_words.bitcast(I32).rearrange("a p w -> p a w"))
         load_tab(1)
-        load_wg(1)
-        nc.sync.dma_start(router[:], wgo)
-        load_gates(0)
-
-        def spread_rows(queue, planes, rows):
-            for q in range(QUADS):
-                queue.dma_start(planes[32 * q : 32 * q + 4, :].bitcast(I32), rows[8 * q : 8 * q + 8, :])
-
-        wu_rows = held("wu_rows", [32, R // 4], I32)
-        nc.vector.tensor_copy(
-            wu_rows[:].rearrange("p (s g w) -> p s g w", s=PACK, w=2),
-            wu_rows_raw[:].rearrange("p (g s w) -> p s g w", s=PACK, w=2),
-        )
-        spread_rows(nc.scalar, wu_planes, wu_rows[:])
 
         tok = [held("tok%d" % a, [P, J], U32) for a in range(PASSES)]
         tok_rows = held("tok_rows", [P, J], U8)
         nc.vector.tensor_copy(tok_rows[:], tab_rows[:].indirect(offsets[:]))
-        spread_rows(nc.gpsimd, tok_planes, tok_rows[:].bitcast(I32))
+        for q in range(QUADS):
+            nc.scalar.dma_start(
+                tok_planes[32 * q : 32 * q + 4, :].bitcast(I32), tok_rows[8 * q : 8 * q + 8, :].bitcast(I32)
+            )
+        load_wg(1, "tab_rows")
         for a in range(PASSES):
             nc.vector.tensor_copy(tok[a][:], tab[a][:].bitcast(U32).indirect(offsets[:]))
-        pages.append(held("page2", [P, T], F32, after="tab0"))
+        router = held("router", [P, J], F32, after="tab0")
+        nc.sync.dma_start(router[:], wgo)
+        for q in range(QUADS):
+            rows = slice(32 * q, 32 * q + 4)
+            nc.vector.tensor_copy(
+                wu_planes[rows, :].bitcast(I32).rearrange("p (a s g w) -> p a s g w", a=PASSES, s=PACK, w=2),
+                wu_planes_raw[rows].rearrange("p a (g s w) -> p a s g w", s=PACK, w=2),
+            )
+        pages.append(held("page2", [P, T], F32, after="tab1"))
         for page in pages:
             nc.vector.memset(page[:], 0.0)
 
@@ -118,6 +120,8 @@ def tile_list_modp_ggelu_gate_kernel(
                 wu[:, a, :].bitcast(I32).rearrange("p (s g w) -> p s g w", s=PACK, w=4),
                 wu_raw[:, a, :].rearrange("p (g s w) -> p s g w", s=PACK, w=4),
             )
+
+        load_gates(0, "wu_planes_raw")
 
         wg_codes = [held("wg_codes%d" % a, [P, R], U32) for a in range(PASSES)]
         wg_plane = [held("wg_plane%d" % a, [P, R], U8) for a in range(PASSES)]
@@ -135,14 +139,14 @@ def tile_list_modp_ggelu_gate_kernel(
                         in_=wg_bf[:, K_PASS * (s - 1) : K_PASS * (s + 1)],
                     )
 
-        load_gates(1, after="wg_raw0")
-        wd_raw = held("wd_raw", [P, PACK, N], F32, after="tab1")
+        load_gates(1, "wg_raw0")
+        wd_raw = held("wd_raw", [P, PACK, N], F32, after="wg_bf0")
         wd_rows = wd.rearrange("(g s q) n -> s g q n", s=PACK, q=8)
         for s in range(PACK):
             nc.sync.dma_start(wd_raw[:, s, :], wd_rows[s])
-        load_gates(2, after="wg_raw1")
+        load_gates(2, "tab_rows")
         gather_gates(0, "gated0")
-        load_gates(3, after="gates0")
+        load_gates(3, "wu_planes_raw")
         gather_gates(1, "gated1")
 
         wd_codes = held("wd_codes", [P, N], U32)
@@ -156,7 +160,7 @@ def tile_list_modp_ggelu_gate_kernel(
                 nc.scalar.copy(dst[:, u], src[:, u])
             nc.vector.quantize_mx(out=wd_codes[:].bitcast(FP8X4), scales=wd_plane[:], in_=wd_bf[:])
 
-        h_bf = [held("h_bf%d" % u, [P, HALF * PACK], BF16) for u in range(2)]
+        h_bf = [held("h_bf%d" % u, [P, HALF * PACK], BF16, after=("wg_raw0", None)[u]) for u in range(2)]
         h_codes = [held("h_codes%d" % u, [P, HALF], U32) for u in range(2)]
         h_plane = [held("h_plane%d" % u, [P, HALF], U8) for u in range(2)]
         y = [held("y%d" % u, [P, N_TILES, HALF], F32) for u in range(2)]
@@ -193,7 +197,7 @@ def tile_list_modp_ggelu_gate_kernel(
                 lambda a, s: wg_codes[a][:, P * s : P * (s + 1)].bitcast(FP8X4),
                 lambda a, s: wg_plane[a][:, P * s : P * (s + 1)],
             )
-            act = ring.tile([P, P, PACK], F32, name="act", bufs=3)
+            act = ring.tile([P, P, PACK], F32, name="act", bufs=J_TILES)
             nc.scalar.activation(act[:], ga[:].rearrange("p s j -> p j s"), GELU)
             u, place = divmod(jt, J_TILES // 2)
             nc.vector.tensor_tensor(

@@ -24,8 +24,8 @@ QUADS = 4
 HALF = J // 2
 J_TILES = J // P
 N_TILES = N // P
-PAGES = 3
-UP_BANKS = 5
+PAGES = 2
+BANKS = 4
 
 
 def tile_list_modp_ggelu_gate_kernel(
@@ -82,9 +82,9 @@ def tile_list_modp_ggelu_gate_kernel(
             )
         nc.scalar.activation(warm2[:], warm[:], GELU)
         load_tab(0)
-        load_wg(0, "wg_raw0")
         nc.sync.dma_start(wu_raw[:], wu_words.bitcast(I32).rearrange("a p w -> p a w"))
         load_tab(1)
+        load_wg(0, "wg_raw0")
 
         tok = [held("tok%d" % a, [P, J], U32) for a in range(PASSES)]
         tok_rows = held("tok_rows", [P, J], U8)
@@ -94,19 +94,19 @@ def tile_list_modp_ggelu_gate_kernel(
                 tok_planes[32 * q : 32 * q + 4, :].bitcast(I32), tok_rows[8 * q : 8 * q + 8, :].bitcast(I32)
             )
         load_wg(1, "tab_rows")
-        for a in range(PASSES):
-            nc.vector.tensor_copy(tok[a][:], tab[a][:].bitcast(U32).indirect(offsets[:]))
-        router = held("router", [P, J], F32, after="tab0")
-        nc.sync.dma_start(router[:], wgo)
+
+        def listed(u):
+            return offsets[:, (HALF // 16) * u : (HALF // 16) * (u + 1)]
+
+        nc.vector.tensor_copy(tok[0][:], tab[0][:].bitcast(U32).indirect(offsets[:]))
+        load_gates(0, "tab0")
         for q in range(QUADS):
             rows = slice(32 * q, 32 * q + 4)
             nc.vector.tensor_copy(
                 wu_planes[rows, :].bitcast(I32).rearrange("p (a s g w) -> p a s g w", a=PASSES, s=PACK, w=2),
                 wu_planes_raw[rows].rearrange("p a (g s w) -> p a s g w", s=PACK, w=2),
             )
-        pages.append(held("page2", [P, T], F32, after="tab1"))
-        for page in pages:
-            nc.vector.memset(page[:], 0.0)
+        nc.vector.memset(pages[0][:], 0.0)
 
         gated = {}
 
@@ -121,7 +121,12 @@ def tile_list_modp_ggelu_gate_kernel(
                 wu_raw[:, a, :].rearrange("p (g s w) -> p s g w", s=PACK, w=4),
             )
 
-        load_gates(0, "wu_planes_raw")
+        router = held("router", [P, J], F32, after="wu_raw")
+        nc.sync.dma_start(router[:], wgo)
+        for u in range(2):
+            nc.vector.tensor_copy(tok[1][:, HALF * u : HALF * (u + 1)], tab[1][:].bitcast(U32).indirect(listed(u)))
+        pages.append(held("page1", [P, T], F32, after="tab1"))
+        nc.vector.memset(pages[1][:], 0.0)
 
         wg_codes = [held("wg_codes%d" % a, [P, R], U32) for a in range(PASSES)]
         wg_plane = [held("wg_plane%d" % a, [P, R], U8) for a in range(PASSES)]
@@ -130,7 +135,10 @@ def tile_list_modp_ggelu_gate_kernel(
             dst = wg_bf[:].rearrange("p (s g u c i) -> p s g u i c", s=PACK, u=2, c=4, i=PACK)
             src = wg_raw[a][:].rearrange("p i (g s u c) -> p s g u i c", s=PACK, u=2, c=4)
             for s in range(PACK):
-                nc.scalar.copy(dst[:, s], src[:, s])
+                if a == 1 and s < 2:
+                    nc.vector.tensor_copy(dst[:, s], src[:, s])
+                else:
+                    nc.scalar.copy(dst[:, s], src[:, s])
                 if s % 2 == 1:
                     cols = slice(P * (s - 1), P * (s + 1))
                     nc.vector.quantize_mx(
@@ -139,15 +147,14 @@ def tile_list_modp_ggelu_gate_kernel(
                         in_=wg_bf[:, K_PASS * (s - 1) : K_PASS * (s + 1)],
                     )
 
-        load_gates(1, "wg_raw0")
-        wd_raw = held("wd_raw", [P, PACK, N], F32, after="wg_bf0")
+        wd_raw = held("wd_raw", [P, PACK, N], F32, after="wg_raw0")
         wd_rows = wd.rearrange("(g s q) n -> s g q n", s=PACK, q=8)
         for s in range(PACK):
             nc.sync.dma_start(wd_raw[:, s, :], wd_rows[s])
+        load_gates(1, "wg_bf0")
         load_gates(2, "tab_rows")
+        load_gates(3, "wg_bf1")
         gather_gates(0, "gated0")
-        load_gates(3, "wu_planes_raw")
-        gather_gates(1, "gated1")
 
         wd_codes = held("wd_codes", [P, N], U32)
         wd_plane = held("wd_plane", [P, N], U8)
@@ -160,10 +167,10 @@ def tile_list_modp_ggelu_gate_kernel(
                 nc.scalar.copy(dst[:, u], src[:, u])
             nc.vector.quantize_mx(out=wd_codes[:].bitcast(FP8X4), scales=wd_plane[:], in_=wd_bf[:])
 
-        h_bf = [held("h_bf%d" % u, [P, HALF * PACK], BF16, after=("wg_raw0", None)[u]) for u in range(2)]
+        h_bf = [held("h_bf%d" % u, [P, HALF * PACK], BF16) for u in range(2)]
         h_codes = [held("h_codes%d" % u, [P, HALF], U32) for u in range(2)]
         h_plane = [held("h_plane%d" % u, [P, HALF], U8) for u in range(2)]
-        y = [held("y%d" % u, [P, N_TILES, HALF], F32) for u in range(2)]
+        y = [held("y%d" % n, [P, J], F32) for n in range(N_TILES)]
 
         ups = {}
 
@@ -181,7 +188,7 @@ def tile_list_modp_ggelu_gate_kernel(
                     )
 
         def up_product(jt):
-            ups[jt] = psum.tile([P, PACK, P], F32, name="ub", bufs=UP_BANKS)
+            ups[jt] = psum.tile([P, PACK, P], F32, name="ub", tag="early" if jt < BANKS else "late", bufs=BANKS)
             first_product(
                 ups[jt],
                 jt,
@@ -190,7 +197,9 @@ def tile_list_modp_ggelu_gate_kernel(
             )
 
         def first_stage(jt):
-            ga = psum.tile([P, PACK, P], F32, name="ga", bufs=2)
+            if jt >= BANKS:
+                up_product(jt)
+            ga = psum.tile([P, PACK, P], F32, name="ga", tag="late", bufs=BANKS)
             first_product(
                 ga,
                 jt,
@@ -206,13 +215,11 @@ def tile_list_modp_ggelu_gate_kernel(
                 act[:],
                 MULT,
             )
-            if jt + UP_BANKS < J_TILES:
-                up_product(jt + UP_BANKS)
 
         def second_stage(u):
             nc.vector.quantize_mx(out=h_codes[u][:].bitcast(FP8X4), scales=h_plane[u][:], in_=h_bf[u][:])
             for n in range(N_TILES):
-                acc = psum.tile([P, HALF], F32, name="acc", bufs=1)
+                acc = psum.tile([P, HALF], F32, name="acc", tag="early", bufs=BANKS)
                 nc.tensor.matmul_mx(
                     out=acc[:],
                     lhsT=wd_codes[:, P * n : P * (n + 1)].bitcast(FP8X4),
@@ -222,36 +229,35 @@ def tile_list_modp_ggelu_gate_kernel(
                     start=True,
                     stop=True,
                 )
-                nc.scalar.copy(y[u][:, n, :], acc[:])
+                nc.scalar.copy(y[n][:, HALF * u : HALF * (u + 1)], acc[:])
 
-        def scatter(n, u):
-            nc.vector.tensor_tensor(
-                pages[n % PAGES][:].indirect(offsets[:, (HALF // 16) * u : (HALF // 16) * (u + 1)]),
-                y[u][:, n, :],
-                gated[n][:, HALF * u : HALF * (u + 1)],
-                MULT,
-            )
+        def scatter_half(n, u):
+            cols = slice(HALF * u, HALF * (u + 1))
+            nc.vector.tensor_tensor(pages[n % PAGES][:].indirect(listed(u)), y[n][:, cols], gated[n][:, cols], MULT)
+
+        def scatter(n):
+            nc.vector.tensor_tensor(pages[n % PAGES][:].indirect(offsets[:]), y[n][:], gated[n][:], MULT)
 
         def store(n):
             nc.sync.dma_start(out[P * n : P * (n + 1), :], pages[n % PAGES][:])
 
-        for jt in range(UP_BANKS):
+        for jt in range(BANKS):
             up_product(jt)
         for jt in range(J_TILES // 2):
             first_stage(jt)
         quantise_wd()
         second_stage(0)
-        gather_gates(2, "gated2")
         for jt in range(J_TILES // 2, J_TILES):
             first_stage(jt)
         second_stage(1)
-        gather_gates(3, "h_bf1")
+        gather_gates(1, "gated1")
+        gather_gates(2, "h_bf1")
         for u in range(2):
             for n in range(PAGES):
-                scatter(n, u)
+                scatter_half(n, u)
                 if u == 1:
                     store(n)
+        gather_gates(3, "gated0")
         for n in range(PAGES, N_TILES):
-            for u in range(2):
-                scatter(n, u)
+            scatter(n)
             store(n)

@@ -1,6 +1,7 @@
 from contextlib import ExitStack
 
 import concourse.mybir as mybir
+from concourse.masks import make_identity
 
 K, R, N, T, J = 1024, 512, 512, 2048, 1024
 FLOPS = 2 * J * (2 * K * R + R * N)
@@ -35,6 +36,8 @@ def tile_list_modp_ggelu_gate_kernel(
     with ExitStack() as ctx:
         keep = ctx.enter_context(tc.tile_pool(name="keep", bufs=1))
         ring = ctx.enter_context(tc.tile_pool(name="ring", bufs=2))
+        shared = ctx.enter_context(tc.tile_pool(name="shared", bufs=1))
+        early = ctx.enter_context(tc.tile_pool(name="early", bufs=1))
         psum = ctx.enter_context(tc.psum_pool(name="psum", bufs=2))
 
         def held(name, shape, dtype, after=None):
@@ -43,7 +46,7 @@ def tile_list_modp_ggelu_gate_kernel(
         offsets = keep.tile([P, J // 16], U16, name="offsets")
         nc.sync.dma_start(offsets[:], offs)
 
-        tab_rows = held("tab_rows", [P, T], U8)
+        tab_rows = early.tile([P, T], U8, name="tab_rows", offset=4 * T - T // 2, align_bytes=64)
         tok_planes = held("tok_planes", [P, PASSES * J], U8)
         wu_planes = held("wu_planes", [P, PASSES * R], U8)
         nc.vector.memset(tab_rows[32:64, :].bitcast(I32), 0)
@@ -52,8 +55,11 @@ def tile_list_modp_ggelu_gate_kernel(
         nc.vector.memset(wu_planes[:].bitcast(I32), 0)
         warm = held("warm", [P, 1], F32)
         warm2 = held("warm2", [P, 1], F32)
+        router_rows = held("router_rows", [P, P], F32)
+        identity = held("identity", [P, P], F32)
         nc.gpsimd.memset(warm[:], 0.0)
-        pages = [held("page%d" % i, [P, T], F32) for i in range(PAGES - 1)]
+        nc.gpsimd.memset(router_rows[:], 0.0)
+        make_identity(nc, identity[:])
 
         tab = [held("tab%d" % a, [P, T], I32) for a in range(PASSES)]
         gates = {}
@@ -64,12 +70,12 @@ def tile_list_modp_ggelu_gate_kernel(
         def load_tab(a):
             nc.sync.dma_start(tab[a][:], tab_words[a].rearrange("p t i -> p (t i)").bitcast(I32))
 
-        def load_gates(n, after):
-            gates[n] = held("gates%d" % n, [P, T], F32, after)
+        def load_gates(n, tile):
+            gates[n] = tile
             nc.sync.dma_start(gates[n][:], gT[P * n : P * (n + 1), :])
 
-        def load_wg(a, after):
-            wg_raw[a] = held("wg_raw%d" % a, [P, PACK, R], F32, after)
+        def load_wg(a):
+            wg_raw[a] = early.tile([P, PACK, R], F32, name="wg_raw%d" % a, offset=4 * T * a, align_bytes=64)
             nc.sync.dma_start(
                 wg_raw[a][:], wg[K_PASS * a : K_PASS * (a + 1), :].rearrange("(p i) r -> p i r", i=PACK)
             )
@@ -80,11 +86,23 @@ def tile_list_modp_ggelu_gate_kernel(
                 wu_planes_raw[32 * q : 32 * q + 4],
                 wu_scales[:, 4 * q : 4 * q + 4, :].bitcast(I32).rearrange("a p w -> p a w"),
             )
+        nc.scalar.dma_start(router_rows[0:J_TILES, :], wgo[0].rearrange("(c n) -> c n", n=P))
         nc.scalar.activation(warm2[:], warm[:], GELU)
         load_tab(0)
         nc.sync.dma_start(wu_raw[:], wu_words.bitcast(I32).rearrange("a p w -> p a w"))
         load_tab(1)
-        load_wg(0, "wg_raw0")
+
+        router = held("router", [P, J], F32)
+        router_cols = held("router_cols", [P, J_TILES], F32)
+        turned = psum.tile([P, P], F32, name="turned", tag="early", bufs=BANKS)
+        nc.tensor.transpose(turned[:], router_rows[:], identity[:])
+        nc.scalar.copy(router_cols[:], turned[:, 0:J_TILES])
+        for u in range(2):
+            spread = psum.tile([P, PACK, P], F32, name="spread", tag="early", bufs=BANKS)
+            for c in range(PACK):
+                jt = PACK * u + c
+                nc.tensor.transpose(spread[:, c, :], router_cols[:, jt : jt + 1].to_broadcast([P, P]), identity[:])
+            nc.scalar.copy(router[:, HALF * u : HALF * (u + 1)], spread[:].rearrange("p c n -> p (c n)"))
 
         tok = [held("tok%d" % a, [P, J], U32) for a in range(PASSES)]
         tok_rows = held("tok_rows", [P, J], U8)
@@ -93,25 +111,25 @@ def tile_list_modp_ggelu_gate_kernel(
             nc.scalar.dma_start(
                 tok_planes[32 * q : 32 * q + 4, :].bitcast(I32), tok_rows[8 * q : 8 * q + 8, :].bitcast(I32)
             )
-        load_wg(1, "tab_rows")
+        load_wg(0)
+        load_wg(1)
 
         def listed(u):
             return offsets[:, (HALF // 16) * u : (HALF // 16) * (u + 1)]
 
         nc.vector.tensor_copy(tok[0][:], tab[0][:].bitcast(U32).indirect(offsets[:]))
-        load_gates(0, "tab0")
+        load_gates(0, held("gates0", [P, T], F32, after="tab0"))
         for q in range(QUADS):
             rows = slice(32 * q, 32 * q + 4)
             nc.vector.tensor_copy(
                 wu_planes[rows, :].bitcast(I32).rearrange("p (a s g w) -> p a s g w", a=PASSES, s=PACK, w=2),
                 wu_planes_raw[rows].rearrange("p a (g s w) -> p a s g w", s=PACK, w=2),
             )
-        nc.vector.memset(pages[0][:], 0.0)
 
         gated = {}
 
-        def gather_gates(n, tag):
-            gated[n] = keep.tile([P, J], F32, name="gated%d" % n, tag=tag, align_bytes=64)
+        def gather_gates(n, tile):
+            gated[n] = tile
             nc.vector.tensor_tensor(gated[n][:], gates[n][:].indirect(offsets[:]), router[:], MULT)
 
         wu = held("wu", [P, PASSES, 2 * R], U8)
@@ -121,12 +139,10 @@ def tile_list_modp_ggelu_gate_kernel(
                 wu_raw[:, a, :].rearrange("p (g s w) -> p s g w", s=PACK, w=4),
             )
 
-        router = held("router", [P, J], F32, after="wu_raw")
-        nc.sync.dma_start(router[:], wgo)
         for u in range(2):
             nc.vector.tensor_copy(tok[1][:, HALF * u : HALF * (u + 1)], tab[1][:].bitcast(U32).indirect(listed(u)))
-        pages.append(held("page1", [P, T], F32, after="tab1"))
-        nc.vector.memset(pages[1][:], 0.0)
+        pages = [held("page0", [P, T], F32, after="tab1")]
+        nc.vector.memset(pages[0][:], 0.0)
 
         wg_codes = [held("wg_codes%d" % a, [P, R], U32) for a in range(PASSES)]
         wg_plane = [held("wg_plane%d" % a, [P, R], U8) for a in range(PASSES)]
@@ -147,14 +163,14 @@ def tile_list_modp_ggelu_gate_kernel(
                         in_=wg_bf[:, K_PASS * (s - 1) : K_PASS * (s + 1)],
                     )
 
-        wd_raw = held("wd_raw", [P, PACK, N], F32, after="wg_raw0")
+        wd_raw = held("wd_raw", [P, PACK, N], F32, after="wu_raw")
         wd_rows = wd.rearrange("(g s q) n -> s g q n", s=PACK, q=8)
         for s in range(PACK):
             nc.sync.dma_start(wd_raw[:, s, :], wd_rows[s])
-        load_gates(1, "wg_bf0")
-        load_gates(2, "tab_rows")
-        load_gates(3, "wg_bf1")
-        gather_gates(0, "gated0")
+        load_gates(1, early.tile([P, T], F32, name="gates1", offset=0, align_bytes=64))
+        load_gates(2, held("gates2", [P, T], F32, after="wg_bf0"))
+        load_gates(3, held("gates3", [P, T], F32, after="wg_bf1"))
+        gather_gates(0, held("gated0", [P, J], F32))
 
         wd_codes = held("wd_codes", [P, N], U32)
         wd_plane = held("wd_plane", [P, N], U8)
@@ -167,7 +183,10 @@ def tile_list_modp_ggelu_gate_kernel(
                 nc.scalar.copy(dst[:, u], src[:, u])
             nc.vector.quantize_mx(out=wd_codes[:].bitcast(FP8X4), scales=wd_plane[:], in_=wd_bf[:])
 
-        h_bf = [held("h_bf%d" % u, [P, HALF * PACK], BF16) for u in range(2)]
+        h_bf = [
+            held("h_bf0", [P, HALF * PACK], BF16),
+            shared.tile([P, HALF * PACK], BF16, name="h_bf1", offset=4 * T - 2 * J, align_bytes=64),
+        ]
         h_codes = [held("h_codes%d" % u, [P, HALF], U32) for u in range(2)]
         h_plane = [held("h_plane%d" % u, [P, HALF], U8) for u in range(2)]
         y = [held("y%d" % n, [P, J], F32) for n in range(N_TILES)]
@@ -250,14 +269,14 @@ def tile_list_modp_ggelu_gate_kernel(
         for jt in range(J_TILES // 2, J_TILES):
             first_stage(jt)
         second_stage(1)
-        gather_gates(1, "gated1")
-        gather_gates(2, "h_bf1")
+        gather_gates(1, held("gated1", [P, J], F32))
+        pages.append(shared.tile([P, T], F32, name="page1", offset=0, align_bytes=64))
+        nc.gpsimd.memset(pages[1][:], 0.0)
+        gather_gates(2, shared.tile([P, J], F32, name="gated2", offset=4 * T, align_bytes=64))
         for u in range(2):
-            for n in range(PAGES):
-                scatter_half(n, u)
-                if u == 1:
-                    store(n)
-        gather_gates(3, "gated0")
-        for n in range(PAGES, N_TILES):
+            scatter_half(0, u)
+        store(0)
+        gather_gates(3, held("gated3", [P, J], F32, after="gated0"))
+        for n in range(1, N_TILES):
             scatter(n)
             store(n)

@@ -36,7 +36,6 @@ def tile_list_modp_ggelu_gate_kernel(
     with ExitStack() as ctx:
         keep = ctx.enter_context(tc.tile_pool(name="keep", bufs=1))
         ring = ctx.enter_context(tc.tile_pool(name="ring", bufs=2))
-        shared = ctx.enter_context(tc.tile_pool(name="shared", bufs=1))
         early = ctx.enter_context(tc.tile_pool(name="early", bufs=1))
         psum = ctx.enter_context(tc.psum_pool(name="psum", bufs=2))
 
@@ -49,10 +48,11 @@ def tile_list_modp_ggelu_gate_kernel(
         tab_rows = early.tile([P, T], U8, name="tab_rows", offset=4 * T - T // 2, align_bytes=64)
         tok_planes = held("tok_planes", [P, PASSES * J], U8)
         wu_planes = held("wu_planes", [P, PASSES * R], U8)
+        wu_planes_raw = held("wu_planes_raw", [P, PASSES, R // 4], I32)
+        nc.vector.memset(wu_planes_raw[:], 0)
         nc.vector.memset(tab_rows[32:64, :].bitcast(I32), 0)
         nc.vector.memset(tab_rows[64:128, :].bitcast(I32), 0)
         nc.vector.memset(tok_planes[:].bitcast(I32), 0)
-        nc.vector.memset(wu_planes[:].bitcast(I32), 0)
         warm = held("warm", [P, 1], F32)
         warm2 = held("warm2", [P, 1], F32)
         router_rows = held("router_rows", [P, P], F32)
@@ -65,7 +65,6 @@ def tile_list_modp_ggelu_gate_kernel(
         gates = {}
         wg_raw = {}
         wu_raw = held("wu_raw", [P, PASSES, R // 2], I32)
-        wu_planes_raw = held("wu_planes_raw", [P, PASSES, R // 4], I32)
 
         def load_tab(a):
             nc.sync.dma_start(tab[a][:], tab_words[a].rearrange("p t i -> p (t i)").bitcast(I32))
@@ -88,6 +87,8 @@ def tile_list_modp_ggelu_gate_kernel(
             )
         nc.scalar.dma_start(router_rows[0:J_TILES, :], wgo[0].rearrange("(c n) -> c n", n=P))
         nc.scalar.activation(warm2[:], warm[:], GELU)
+        pages = [held("page0", [P, T], F32)]
+        nc.vector.memset(pages[0][:], 0.0)
         load_tab(0)
         nc.sync.dma_start(wu_raw[:], wu_words.bitcast(I32).rearrange("a p w -> p a w"))
         load_tab(1)
@@ -119,12 +120,10 @@ def tile_list_modp_ggelu_gate_kernel(
 
         nc.vector.tensor_copy(tok[0][:], tab[0][:].bitcast(U32).indirect(offsets[:]))
         load_gates(0, held("gates0", [P, T], F32, after="tab0"))
-        for q in range(QUADS):
-            rows = slice(32 * q, 32 * q + 4)
-            nc.vector.tensor_copy(
-                wu_planes[rows, :].bitcast(I32).rearrange("p (a s g w) -> p a s g w", a=PASSES, s=PACK, w=2),
-                wu_planes_raw[rows].rearrange("p a (g s w) -> p a s g w", s=PACK, w=2),
-            )
+        nc.vector.tensor_copy(
+            wu_planes[:].bitcast(I32).rearrange("p (a s g w) -> p a s g w", a=PASSES, s=PACK, w=2),
+            wu_planes_raw[:].rearrange("p a (g s w) -> p a s g w", s=PACK, w=2),
+        )
 
         gated = {}
 
@@ -133,16 +132,15 @@ def tile_list_modp_ggelu_gate_kernel(
             nc.vector.tensor_tensor(gated[n][:], gates[n][:].indirect(offsets[:]), router[:], MULT)
 
         wu = held("wu", [P, PASSES, 2 * R], U8)
-        for a in range(PASSES):
-            nc.vector.tensor_copy(
-                wu[:, a, :].bitcast(I32).rearrange("p (s g w) -> p s g w", s=PACK, w=4),
-                wu_raw[:, a, :].rearrange("p (g s w) -> p s g w", s=PACK, w=4),
-            )
+        nc.vector.tensor_copy(
+            wu[:].bitcast(I32).rearrange("p a (s g w) -> p a s g w", s=PACK, w=4),
+            wu_raw[:].rearrange("p a (g s w) -> p a s g w", s=PACK, w=4),
+        )
 
         for u in range(2):
             nc.vector.tensor_copy(tok[1][:, HALF * u : HALF * (u + 1)], tab[1][:].bitcast(U32).indirect(listed(u)))
-        pages = [held("page0", [P, T], F32, after="tab1")]
-        nc.vector.memset(pages[0][:], 0.0)
+        pages.append(held("page1", [P, T], F32, after="tab1"))
+        nc.vector.memset(pages[1][:], 0.0)
 
         wg_codes = [held("wg_codes%d" % a, [P, R], U32) for a in range(PASSES)]
         wg_plane = [held("wg_plane%d" % a, [P, R], U8) for a in range(PASSES)]
@@ -183,10 +181,7 @@ def tile_list_modp_ggelu_gate_kernel(
                 nc.scalar.copy(dst[:, u], src[:, u])
             nc.vector.quantize_mx(out=wd_codes[:].bitcast(FP8X4), scales=wd_plane[:], in_=wd_bf[:])
 
-        h_bf = [
-            held("h_bf0", [P, HALF * PACK], BF16),
-            shared.tile([P, HALF * PACK], BF16, name="h_bf1", offset=4 * T - 2 * J, align_bytes=64),
-        ]
+        h_bf = [held("h_bf%d" % u, [P, HALF * PACK], BF16) for u in range(2)]
         h_codes = [held("h_codes%d" % u, [P, HALF], U32) for u in range(2)]
         h_plane = [held("h_plane%d" % u, [P, HALF], U8) for u in range(2)]
         y = [held("y%d" % n, [P, J], F32) for n in range(N_TILES)]
@@ -270,13 +265,12 @@ def tile_list_modp_ggelu_gate_kernel(
             first_stage(jt)
         second_stage(1)
         gather_gates(1, held("gated1", [P, J], F32))
-        pages.append(shared.tile([P, T], F32, name="page1", offset=0, align_bytes=64))
-        nc.gpsimd.memset(pages[1][:], 0.0)
-        gather_gates(2, shared.tile([P, J], F32, name="gated2", offset=4 * T, align_bytes=64))
+        gather_gates(2, held("gated2", [P, J], F32, after="h_bf1"))
         for u in range(2):
             scatter_half(0, u)
         store(0)
-        gather_gates(3, held("gated3", [P, J], F32, after="gated0"))
         for n in range(1, N_TILES):
             scatter(n)
             store(n)
+            if n == 1:
+                gather_gates(3, held("gated3", [P, J], F32, after="gated0"))

@@ -37,6 +37,7 @@ def tile_list_modp_ggelu_gate_kernel(
         keep = ctx.enter_context(tc.tile_pool(name="keep", bufs=1))
         ring = ctx.enter_context(tc.tile_pool(name="ring", bufs=2))
         early = ctx.enter_context(tc.tile_pool(name="early", bufs=1))
+        paged = ctx.enter_context(tc.tile_pool(name="paged", bufs=1))
         psum = ctx.enter_context(tc.psum_pool(name="psum", bufs=2))
 
         def held(name, shape, dtype, after=None):
@@ -49,19 +50,19 @@ def tile_list_modp_ggelu_gate_kernel(
         tok_planes = held("tok_planes", [P, PASSES * J], U8)
         wu_planes = held("wu_planes", [P, PASSES * R], U8)
         wu_planes_raw = held("wu_planes_raw", [P, PASSES, R // 4], I32)
+        router_rows = held("router_rows", [P, P], F32)
+        nc.vector.memset(router_rows[:], 0.0)
         nc.vector.memset(wu_planes_raw[:], 0)
         nc.vector.memset(tab_rows[32:64, :].bitcast(I32), 0)
         nc.vector.memset(tab_rows[64:128, :].bitcast(I32), 0)
         nc.vector.memset(tok_planes[:].bitcast(I32), 0)
-        warm = held("warm", [P, 1], F32)
-        warm2 = held("warm2", [P, 1], F32)
-        router_rows = held("router_rows", [P, P], F32)
         identity = held("identity", [P, P], F32)
-        nc.gpsimd.memset(warm[:], 0.0)
-        nc.gpsimd.memset(router_rows[:], 0.0)
         make_identity(nc, identity[:])
 
-        tab = [held("tab%d" % a, [P, T], I32) for a in range(PASSES)]
+        tab = [
+            held("tab0", [P, T], I32),
+            paged.tile([P, T], I32, name="tab1", offset=2 * T, align_bytes=64),
+        ]
         gates = {}
         wg_raw = {}
         wu_raw = held("wu_raw", [P, PASSES, R // 2], I32)
@@ -86,9 +87,6 @@ def tile_list_modp_ggelu_gate_kernel(
                 wu_scales[:, 4 * q : 4 * q + 4, :].bitcast(I32).rearrange("a p w -> p a w"),
             )
         nc.scalar.dma_start(router_rows[0:J_TILES, :], wgo[0].rearrange("(c n) -> c n", n=P))
-        nc.scalar.activation(warm2[:], warm[:], GELU)
-        pages = [held("page0", [P, T], F32)]
-        nc.vector.memset(pages[0][:], 0.0)
         load_tab(0)
         nc.sync.dma_start(wu_raw[:], wu_words.bitcast(I32).rearrange("a p w -> p a w"))
         load_tab(1)
@@ -139,8 +137,9 @@ def tile_list_modp_ggelu_gate_kernel(
 
         for u in range(2):
             nc.vector.tensor_copy(tok[1][:, HALF * u : HALF * (u + 1)], tab[1][:].bitcast(U32).indirect(listed(u)))
-        pages.append(held("page1", [P, T], F32, after="tab1"))
-        nc.vector.memset(pages[1][:], 0.0)
+        pages = [paged.tile([P, T], F32, name="page%d" % i, offset=4 * T * i, align_bytes=64) for i in range(PAGES)]
+        for page in pages:
+            nc.vector.memset(page[:].bitcast(I32), 0)
 
         wg_codes = [held("wg_codes%d" % a, [P, R], U32) for a in range(PASSES)]
         wg_plane = [held("wg_plane%d" % a, [P, R], U8) for a in range(PASSES)]
@@ -149,10 +148,7 @@ def tile_list_modp_ggelu_gate_kernel(
             dst = wg_bf[:].rearrange("p (s g u c i) -> p s g u i c", s=PACK, u=2, c=4, i=PACK)
             src = wg_raw[a][:].rearrange("p i (g s u c) -> p s g u i c", s=PACK, u=2, c=4)
             for s in range(PACK):
-                if a == 1 and s < 2:
-                    nc.vector.tensor_copy(dst[:, s], src[:, s])
-                else:
-                    nc.scalar.copy(dst[:, s], src[:, s])
+                nc.scalar.copy(dst[:, s], src[:, s])
                 if s % 2 == 1:
                     cols = slice(P * (s - 1), P * (s + 1))
                     nc.vector.quantize_mx(
@@ -161,14 +157,15 @@ def tile_list_modp_ggelu_gate_kernel(
                         in_=wg_bf[:, K_PASS * (s - 1) : K_PASS * (s + 1)],
                     )
 
-        wd_raw = held("wd_raw", [P, PACK, N], F32, after="wu_raw")
+        load_gates(1, held("gates1", [P, T], F32, after="wu_raw"))
+        wd_raw = early.tile([P, PACK, N], F32, name="wd_raw", offset=0, align_bytes=64)
         wd_rows = wd.rearrange("(g s q) n -> s g q n", s=PACK, q=8)
         for s in range(PACK):
             nc.sync.dma_start(wd_raw[:, s, :], wd_rows[s])
-        load_gates(1, early.tile([P, T], F32, name="gates1", offset=0, align_bytes=64))
         load_gates(2, held("gates2", [P, T], F32, after="wg_bf0"))
-        load_gates(3, held("gates3", [P, T], F32, after="wg_bf1"))
-        gather_gates(0, held("gated0", [P, J], F32))
+        load_gates(3, early.tile([P, T], F32, name="gates3", offset=4 * T, align_bytes=64))
+        for n in range(N_TILES - 1):
+            gather_gates(n, held("gated%d" % n, [P, J], F32))
 
         wd_codes = held("wd_codes", [P, N], U32)
         wd_plane = held("wd_plane", [P, N], U8)
@@ -264,13 +261,10 @@ def tile_list_modp_ggelu_gate_kernel(
         for jt in range(J_TILES // 2, J_TILES):
             first_stage(jt)
         second_stage(1)
-        gather_gates(1, held("gated1", [P, J], F32))
-        gather_gates(2, held("gated2", [P, J], F32, after="h_bf1"))
+        gather_gates(3, held("gated3", [P, J], F32, after="h_bf1"))
         for u in range(2):
             scatter_half(0, u)
         store(0)
         for n in range(1, N_TILES):
             scatter(n)
             store(n)
-            if n == 1:
-                gather_gates(3, held("gated3", [P, J], F32, after="gated0"))

@@ -1,7 +1,6 @@
 from contextlib import ExitStack
 
 import concourse.mybir as mybir
-from concourse.masks import make_identity
 
 K, R, N, T, J = 1024, 512, 512, 2048, 1024
 FLOPS = 2 * J * (2 * K * R + R * N)
@@ -35,7 +34,6 @@ def tile_list_modp_ggelu_gate_kernel(
     nc = tc.nc
     with ExitStack() as ctx:
         keep = ctx.enter_context(tc.tile_pool(name="keep", bufs=1))
-        ring = ctx.enter_context(tc.tile_pool(name="ring", bufs=2))
         early = ctx.enter_context(tc.tile_pool(name="early", bufs=1))
         paged = ctx.enter_context(tc.tile_pool(name="paged", bufs=1))
         psum = ctx.enter_context(tc.psum_pool(name="psum", bufs=2))
@@ -50,18 +48,16 @@ def tile_list_modp_ggelu_gate_kernel(
         tok_planes = held("tok_planes", [P, PASSES * J], U8)
         wu_planes = held("wu_planes", [P, PASSES * R], U8)
         wu_planes_raw = held("wu_planes_raw", [P, PASSES, R // 4], I32)
-        router_rows = held("router_rows", [P, P], F32)
-        nc.vector.memset(router_rows[:], 0.0)
         nc.vector.memset(wu_planes_raw[:], 0)
         nc.vector.memset(tab_rows[32:64, :].bitcast(I32), 0)
         nc.vector.memset(tab_rows[64:128, :].bitcast(I32), 0)
         nc.vector.memset(tok_planes[:].bitcast(I32), 0)
-        identity = held("identity", [P, P], F32)
-        make_identity(nc, identity[:])
+        pages = [held("page0", [P, T], F32)]
+        nc.vector.memset(pages[0][:].bitcast(I32), 0)
 
         tab = [
-            held("tab0", [P, T], I32),
-            paged.tile([P, T], I32, name="tab1", offset=2 * T, align_bytes=64),
+            paged.tile([P, T], I32, name="tab0", offset=3 * T, align_bytes=64),
+            held("tab1", [P, T], I32),
         ]
         gates = {}
         wg_raw = {}
@@ -86,22 +82,9 @@ def tile_list_modp_ggelu_gate_kernel(
                 wu_planes_raw[32 * q : 32 * q + 4],
                 wu_scales[:, 4 * q : 4 * q + 4, :].bitcast(I32).rearrange("a p w -> p a w"),
             )
-        nc.scalar.dma_start(router_rows[0:J_TILES, :], wgo[0].rearrange("(c n) -> c n", n=P))
         load_tab(0)
         nc.sync.dma_start(wu_raw[:], wu_words.bitcast(I32).rearrange("a p w -> p a w"))
         load_tab(1)
-
-        router = held("router", [P, J], F32)
-        router_cols = held("router_cols", [P, J_TILES], F32)
-        turned = psum.tile([P, P], F32, name="turned", tag="early", bufs=BANKS)
-        nc.tensor.transpose(turned[:], router_rows[:], identity[:])
-        nc.scalar.copy(router_cols[:], turned[:, 0:J_TILES])
-        for u in range(2):
-            spread = psum.tile([P, PACK, P], F32, name="spread", tag="early", bufs=BANKS)
-            for c in range(PACK):
-                jt = PACK * u + c
-                nc.tensor.transpose(spread[:, c, :], router_cols[:, jt : jt + 1].to_broadcast([P, P]), identity[:])
-            nc.scalar.copy(router[:, HALF * u : HALF * (u + 1)], spread[:].rearrange("p c n -> p (c n)"))
 
         tok = [held("tok%d" % a, [P, J], U32) for a in range(PASSES)]
         tok_rows = held("tok_rows", [P, J], U8)
@@ -117,7 +100,9 @@ def tile_list_modp_ggelu_gate_kernel(
             return offsets[:, (HALF // 16) * u : (HALF // 16) * (u + 1)]
 
         nc.vector.tensor_copy(tok[0][:], tab[0][:].bitcast(U32).indirect(offsets[:]))
-        load_gates(0, held("gates0", [P, T], F32, after="tab0"))
+        router = paged.tile([P, J], F32, name="router", offset=4 * T, align_bytes=64)
+        nc.sync.dma_start(router[:], wgo)
+        load_gates(0, paged.tile([P, T], F32, name="gates0", offset=4 * T + 4 * J, align_bytes=64))
         nc.vector.tensor_copy(
             wu_planes[:].bitcast(I32).rearrange("p (a s g w) -> p a s g w", a=PASSES, s=PACK, w=2),
             wu_planes_raw[:].rearrange("p a (g s w) -> p a s g w", s=PACK, w=2),
@@ -137,9 +122,8 @@ def tile_list_modp_ggelu_gate_kernel(
 
         for u in range(2):
             nc.vector.tensor_copy(tok[1][:, HALF * u : HALF * (u + 1)], tab[1][:].bitcast(U32).indirect(listed(u)))
-        pages = [paged.tile([P, T], F32, name="page%d" % i, offset=4 * T * i, align_bytes=64) for i in range(PAGES)]
-        for page in pages:
-            nc.vector.memset(page[:].bitcast(I32), 0)
+        pages.append(paged.tile([P, T], F32, name="page1", offset=0, align_bytes=64))
+        nc.vector.memset(pages[1][:].bitcast(I32), 0)
 
         wg_codes = [held("wg_codes%d" % a, [P, R], U32) for a in range(PASSES)]
         wg_plane = [held("wg_plane%d" % a, [P, R], U8) for a in range(PASSES)]
@@ -217,7 +201,7 @@ def tile_list_modp_ggelu_gate_kernel(
                 lambda a, s: wg_codes[a][:, P * s : P * (s + 1)].bitcast(FP8X4),
                 lambda a, s: wg_plane[a][:, P * s : P * (s + 1)],
             )
-            act = ring.tile([P, P, PACK], F32, name="act", bufs=J_TILES)
+            act = held("act%d" % jt, [P, P, PACK], F32)
             nc.scalar.activation(act[:], ga[:].rearrange("p s j -> p j s"), GELU)
             u, place = divmod(jt, J_TILES // 2)
             nc.vector.tensor_tensor(
@@ -261,10 +245,14 @@ def tile_list_modp_ggelu_gate_kernel(
         for jt in range(J_TILES // 2, J_TILES):
             first_stage(jt)
         second_stage(1)
-        gather_gates(3, held("gated3", [P, J], F32, after="h_bf1"))
+        gather_gates(3, held("gated3", [P, J], F32, after="act%d" % (J_TILES - 1)))
         for u in range(2):
             scatter_half(0, u)
         store(0)
-        for n in range(1, N_TILES):
+        for n in range(1, N_TILES - 1):
             scatter(n)
             store(n)
+        last = N_TILES - 1
+        scatter(last)
+        for queue, cols in ((nc.sync, slice(0, T // 2)), (nc.scalar, slice(T // 2, T))):
+            queue.dma_start(out[P * last : P * (last + 1), cols], pages[last % PAGES][:, cols])

@@ -90,7 +90,7 @@ def tile_list_modp_ggelu_gate_kernel(
         tok_rows = held("tok_rows", [P, J], U8)
         nc.vector.tensor_copy(tok_rows[:], tab_rows[:].indirect(offsets[:]))
         for q in range(QUADS):
-            nc.scalar.dma_start(
+            nc.sync.dma_start(
                 tok_planes[32 * q : 32 * q + 4, :].bitcast(I32), tok_rows[8 * q : 8 * q + 8, :].bitcast(I32)
             )
         load_wg(0)

@@ -36,7 +36,7 @@ def tile_list_modp_ggelu_gate_kernel(
         keep = ctx.enter_context(tc.tile_pool(name="keep", bufs=1))
         early = ctx.enter_context(tc.tile_pool(name="early", bufs=1))
         paged = ctx.enter_context(tc.tile_pool(name="paged", bufs=1))
-        psum = ctx.enter_context(tc.psum_pool(name="psum", bufs=2))
+        psum = ctx.enter_context(tc.psum_pool(name="psum", bufs=BANKS))
 
         def held(name, shape, dtype, after=None):
             return keep.tile(shape, dtype, name=name, tag=after or name, align_bytes=64)
@@ -44,84 +44,68 @@ def tile_list_modp_ggelu_gate_kernel(
         offsets = keep.tile([P, J // 16], U16, name="offsets")
         nc.sync.dma_start(offsets[:], offs)
 
+        def listed(start, stop):
+            return offsets[:, start // 16 : stop // 16]
+
         tab_rows = early.tile([P, T], U8, name="tab_rows", offset=4 * T - T // 2, align_bytes=64)
         tok_planes = held("tok_planes", [P, PASSES * J], U8)
         wu_planes = held("wu_planes", [P, PASSES * R], U8)
         wu_planes_raw = held("wu_planes_raw", [P, PASSES, R // 4], I32)
         nc.vector.memset(wu_planes_raw[:], 0)
-        nc.vector.memset(tab_rows[32:64, :].bitcast(I32), 0)
-        nc.vector.memset(tab_rows[64:128, :].bitcast(I32), 0)
+        nc.vector.memset(tab_rows[0:96, :].bitcast(I32), 0)
         nc.vector.memset(tok_planes[:].bitcast(I32), 0)
         pages = [held("page0", [P, T], F32)]
         nc.vector.memset(pages[0][:].bitcast(I32), 0)
 
-        tab = [
-            paged.tile([P, T], I32, name="tab0", offset=3 * T, align_bytes=64),
-            held("tab1", [P, T], I32),
-        ]
+        tab = {}
         gates = {}
         wg_raw = {}
-        wu_raw = held("wu_raw", [P, PASSES, R // 2], I32)
 
         def load_tab(a):
+            tab[a] = paged.tile([P, T], I32, name="tab%d" % a, offset=2 * T * (a + 1), align_bytes=64)
             nc.sync.dma_start(tab[a][:], tab_words[a].rearrange("p t i -> p (t i)").bitcast(I32))
 
-        def load_gates(n, tile):
-            gates[n] = tile
+        def load_gates(n, after):
+            gates[n] = held("gates%d" % n, [P, T], F32, after=after)
             nc.sync.dma_start(gates[n][:], gT[P * n : P * (n + 1), :])
 
-        def load_wg(a):
-            wg_raw[a] = early.tile([P, PACK, R], F32, name="wg_raw%d" % a, offset=4 * T * a, align_bytes=64)
-            nc.sync.dma_start(
-                wg_raw[a][:], wg[K_PASS * a : K_PASS * (a + 1), :].rearrange("(p i) r -> p i r", i=PACK)
-            )
+        def load_wg(a, tile):
+            wg_raw[a] = tile
+            nc.sync.dma_start(tile[:], wg[K_PASS * a : K_PASS * (a + 1), :].rearrange("(p i) r -> p i r", i=PACK))
 
-        nc.sync.dma_start(tab_rows[0:32, :].bitcast(I32), tab_scales.bitcast(I32).rearrange("a b w -> b a w"))
+        nc.sync.dma_start(tab_rows[96:128, :].bitcast(I32), tab_scales.bitcast(I32).rearrange("a b w -> b a w"))
         for q in range(QUADS):
             nc.scalar.dma_start(
                 wu_planes_raw[32 * q : 32 * q + 4],
                 wu_scales[:, 4 * q : 4 * q + 4, :].bitcast(I32).rearrange("a p w -> p a w"),
             )
         load_tab(0)
+        wu_raw = held("wu_raw", [P, PASSES, R // 2], I32)
         nc.sync.dma_start(wu_raw[:], wu_words.bitcast(I32).rearrange("a p w -> p a w"))
-        load_tab(1)
+        load_wg(0, held("wg_raw0", [P, PACK, R], F32))
 
         tok = [held("tok%d" % a, [P, J], U32) for a in range(PASSES)]
         tok_rows = held("tok_rows", [P, J], U8)
         nc.vector.tensor_copy(tok_rows[:], tab_rows[:].indirect(offsets[:]))
         for q in range(QUADS):
             nc.sync.dma_start(
-                tok_planes[32 * q : 32 * q + 4, :].bitcast(I32), tok_rows[8 * q : 8 * q + 8, :].bitcast(I32)
+                tok_planes[32 * q : 32 * q + 4, :].bitcast(I32), tok_rows[96 + 8 * q : 96 + 8 * q + 8, :].bitcast(I32)
             )
-        load_wg(0)
-        load_wg(1)
-
-        def listed(u):
-            return offsets[:, (HALF // 16) * u : (HALF // 16) * (u + 1)]
-
+        load_wg(1, early.tile([P, PACK, R], F32, name="wg_raw1", offset=0, align_bytes=64))
         nc.vector.tensor_copy(tok[0][:], tab[0][:].bitcast(U32).indirect(offsets[:]))
-        router = paged.tile([P, J], F32, name="router", offset=4 * T, align_bytes=64)
-        nc.sync.dma_start(router[:], wgo)
-        load_gates(0, paged.tile([P, T], F32, name="gates0", offset=4 * T + 4 * J, align_bytes=64))
+        load_tab(1)
+
         nc.vector.tensor_copy(
             wu_planes[:].bitcast(I32).rearrange("p (a s g w) -> p a s g w", a=PASSES, s=PACK, w=2),
             wu_planes_raw[:].rearrange("p a (g s w) -> p a s g w", s=PACK, w=2),
         )
-
-        gated = {}
-
-        def gather_gates(n, tile):
-            gated[n] = tile
-            nc.vector.tensor_tensor(gated[n][:], gates[n][:].indirect(offsets[:]), router[:], MULT)
-
         wu = held("wu", [P, PASSES, 2 * R], U8)
         nc.vector.tensor_copy(
             wu[:].bitcast(I32).rearrange("p a (s g w) -> p a s g w", s=PACK, w=4),
             wu_raw[:].rearrange("p a (g s w) -> p a s g w", s=PACK, w=4),
         )
-
-        for u in range(2):
-            nc.vector.tensor_copy(tok[1][:, HALF * u : HALF * (u + 1)], tab[1][:].bitcast(U32).indirect(listed(u)))
+        router = held("router", [P, J], F32, after="wu_raw")
+        nc.sync.dma_start(router[:], wgo)
         pages.append(paged.tile([P, T], F32, name="page1", offset=0, align_bytes=64))
         nc.vector.memset(pages[1][:].bitcast(I32), 0)
 
@@ -132,24 +116,96 @@ def tile_list_modp_ggelu_gate_kernel(
             dst = wg_bf[:].rearrange("p (s g u c i) -> p s g u i c", s=PACK, u=2, c=4, i=PACK)
             src = wg_raw[a][:].rearrange("p i (g s u c) -> p s g u i c", s=PACK, u=2, c=4)
             for s in range(PACK):
-                nc.scalar.copy(dst[:, s], src[:, s])
-                if s % 2 == 1:
-                    cols = slice(P * (s - 1), P * (s + 1))
-                    nc.vector.quantize_mx(
-                        out=wg_codes[a][:, cols].bitcast(FP8X4),
-                        scales=wg_plane[a][:, cols],
-                        in_=wg_bf[:, K_PASS * (s - 1) : K_PASS * (s + 1)],
-                    )
+                if a == PASSES - 1 and s >= PACK // 2:
+                    nc.vector.tensor_copy(dst[:, s], src[:, s])
+                else:
+                    nc.scalar.copy(dst[:, s], src[:, s])
+            for s in range(0, PACK, 2):
+                cols = slice(P * s, P * (s + 2))
+                nc.vector.quantize_mx(
+                    out=wg_codes[a][:, cols].bitcast(FP8X4),
+                    scales=wg_plane[a][:, cols],
+                    in_=wg_bf[:, K_PASS * s : K_PASS * (s + 2)],
+                )
 
-        load_gates(1, held("gates1", [P, T], F32, after="wu_raw"))
-        wd_raw = early.tile([P, PACK, N], F32, name="wd_raw", offset=0, align_bytes=64)
+        load_gates(0, "wg_raw0")
+        wd_raw = held("wd_raw", [P, PACK, N], F32, after="wg_bf0")
         wd_rows = wd.rearrange("(g s q) n -> s g q n", s=PACK, q=8)
         for s in range(PACK):
             nc.sync.dma_start(wd_raw[:, s, :], wd_rows[s])
-        load_gates(2, held("gates2", [P, T], F32, after="wg_bf0"))
-        load_gates(3, early.tile([P, T], F32, name="gates3", offset=4 * T, align_bytes=64))
-        for n in range(N_TILES - 1):
-            gather_gates(n, held("gated%d" % n, [P, J], F32))
+        gates[1] = early.tile([P, T], F32, name="gates1", offset=0, align_bytes=64)
+        nc.sync.dma_start(gates[1][:], gT[P : 2 * P, :])
+
+        ups = {}
+        gas = {}
+        acts = {}
+        gated = {}
+        h_bf = {}
+        h_codes = [held("h_codes%d" % u, [P, HALF], U32) for u in range(2)]
+        h_plane = [held("h_plane%d" % u, [P, HALF], U8) for u in range(2)]
+        y = [held("y%d" % n, [P, J], F32) for n in range(N_TILES)]
+
+        def first_pass(acc, jt, a, weights, planes):
+            for s in range(PACK):
+                nc.tensor.matmul_mx(
+                    out=acc[:, s, :],
+                    lhsT=weights(s),
+                    lhsT_scale=planes(s),
+                    rhs=tok[a][:, P * jt : P * (jt + 1)].bitcast(FP8X4),
+                    rhs_scale=tok_planes[:, J * a + P * jt : J * a + P * (jt + 1)],
+                    start=(a == 0 and s == 0),
+                    stop=(a == PASSES - 1 and s == PACK - 1),
+                )
+
+        def up_pass(jt, a):
+            if a == 0:
+                ups[jt] = psum.tile([P, PACK, P], F32, name="ub", tag="up")
+            first_pass(
+                ups[jt],
+                jt,
+                a,
+                lambda s: wu[:, a, 2 * P * s : 2 * P * (s + 1)].bitcast(FP4X4),
+                lambda s: wu_planes[:, R * a + P * s : R * a + P * (s + 1)],
+            )
+
+        def gate_pass(jt, a):
+            if a == 0:
+                gas[jt] = psum.tile([P, PACK, P], F32, name="ga", tag="gate")
+            first_pass(
+                gas[jt],
+                jt,
+                a,
+                lambda s: wg_codes[a][:, P * s : P * (s + 1)].bitcast(FP8X4),
+                lambda s: wg_plane[a][:, P * s : P * (s + 1)],
+            )
+
+        def finish_tile(jt):
+            if jt >= BANKS:
+                gate_pass(jt, 0)
+            gate_pass(jt, 1)
+            acts[jt] = held("act%d" % jt, [P, P, PACK], F32)
+            nc.scalar.activation(acts[jt][:], gas[jt][:].rearrange("p s j -> p j s"), GELU)
+            if jt >= BANKS:
+                up_pass(jt, 0)
+            up_pass(jt, 1)
+
+        def product(jt):
+            pair, place = divmod(jt, 2)
+            nc.vector.tensor_tensor(
+                h_bf[pair][:, K_PASS * place : K_PASS * (place + 1)].rearrange("p (j s) -> p j s", s=PACK),
+                ups[jt][:].rearrange("p s j -> p j s"),
+                acts[jt][:],
+                MULT,
+            )
+
+        def quantise_h(pair):
+            u, place = divmod(pair, 2)
+            cols = slice(2 * P * place, 2 * P * (place + 1))
+            nc.vector.quantize_mx(out=h_codes[u][:, cols].bitcast(FP8X4), scales=h_plane[u][:, cols], in_=h_bf[pair][:])
+
+        def gather_gates(n, tile):
+            gated[n] = tile
+            nc.vector.tensor_tensor(gated[n][:], gates[n][:].indirect(offsets[:]), router[:], MULT)
 
         wd_codes = held("wd_codes", [P, N], U32)
         wd_plane = held("wd_plane", [P, N], U8)
@@ -162,59 +218,9 @@ def tile_list_modp_ggelu_gate_kernel(
                 nc.scalar.copy(dst[:, u], src[:, u])
             nc.vector.quantize_mx(out=wd_codes[:].bitcast(FP8X4), scales=wd_plane[:], in_=wd_bf[:])
 
-        h_bf = [held("h_bf%d" % u, [P, HALF * PACK], BF16) for u in range(2)]
-        h_codes = [held("h_codes%d" % u, [P, HALF], U32) for u in range(2)]
-        h_plane = [held("h_plane%d" % u, [P, HALF], U8) for u in range(2)]
-        y = [held("y%d" % n, [P, J], F32) for n in range(N_TILES)]
-
-        ups = {}
-
-        def first_product(acc, jt, weights, planes):
-            for s in range(PACK):
-                for a in range(PASSES):
-                    nc.tensor.matmul_mx(
-                        out=acc[:, s, :],
-                        lhsT=weights(a, s),
-                        lhsT_scale=planes(a, s),
-                        rhs=tok[a][:, P * jt : P * (jt + 1)].bitcast(FP8X4),
-                        rhs_scale=tok_planes[:, J * a + P * jt : J * a + P * (jt + 1)],
-                        start=(a == 0),
-                        stop=(a == PASSES - 1),
-                    )
-
-        def up_product(jt):
-            ups[jt] = psum.tile([P, PACK, P], F32, name="ub", tag="early" if jt < BANKS else "late", bufs=BANKS)
-            first_product(
-                ups[jt],
-                jt,
-                lambda a, s: wu[:, a, 2 * P * s : 2 * P * (s + 1)].bitcast(FP4X4),
-                lambda a, s: wu_planes[:, R * a + P * s : R * a + P * (s + 1)],
-            )
-
-        def first_stage(jt):
-            if jt >= BANKS:
-                up_product(jt)
-            ga = psum.tile([P, PACK, P], F32, name="ga", tag="late", bufs=BANKS)
-            first_product(
-                ga,
-                jt,
-                lambda a, s: wg_codes[a][:, P * s : P * (s + 1)].bitcast(FP8X4),
-                lambda a, s: wg_plane[a][:, P * s : P * (s + 1)],
-            )
-            act = held("act%d" % jt, [P, P, PACK], F32)
-            nc.scalar.activation(act[:], ga[:].rearrange("p s j -> p j s"), GELU)
-            u, place = divmod(jt, J_TILES // 2)
-            nc.vector.tensor_tensor(
-                h_bf[u][:, K_PASS * place : K_PASS * (place + 1)].rearrange("p (j s) -> p j s", s=PACK),
-                ups[jt][:].rearrange("p s j -> p j s"),
-                act[:],
-                MULT,
-            )
-
         def second_stage(u):
-            nc.vector.quantize_mx(out=h_codes[u][:].bitcast(FP8X4), scales=h_plane[u][:], in_=h_bf[u][:])
             for n in range(N_TILES):
-                acc = psum.tile([P, HALF], F32, name="acc", tag="early", bufs=BANKS)
+                acc = psum.tile([P, HALF], F32, name="acc", tag="gate")
                 nc.tensor.matmul_mx(
                     out=acc[:],
                     lhsT=wd_codes[:, P * n : P * (n + 1)].bitcast(FP8X4),
@@ -226,33 +232,55 @@ def tile_list_modp_ggelu_gate_kernel(
                 )
                 nc.scalar.copy(y[n][:, HALF * u : HALF * (u + 1)], acc[:])
 
-        def scatter_half(n, u):
-            cols = slice(HALF * u, HALF * (u + 1))
-            nc.vector.tensor_tensor(pages[n % PAGES][:].indirect(listed(u)), y[n][:, cols], gated[n][:, cols], MULT)
-
-        def scatter(n):
-            nc.vector.tensor_tensor(pages[n % PAGES][:].indirect(offsets[:]), y[n][:], gated[n][:], MULT)
+        def scatter(n, start, stop):
+            nc.vector.tensor_tensor(
+                pages[n % PAGES][:].indirect(listed(start, stop)), y[n][:, start:stop], gated[n][:, start:stop], MULT
+            )
 
         def store(n):
             nc.sync.dma_start(out[P * n : P * (n + 1), :], pages[n % PAGES][:])
 
         for jt in range(BANKS):
-            up_product(jt)
-        for jt in range(J_TILES // 2):
-            first_stage(jt)
+            up_pass(jt, 0)
+        for jt in range(BANKS):
+            gate_pass(jt, 0)
+        for start, stop in ((0, 2 * P), (2 * P, HALF), (HALF, J)):
+            nc.vector.tensor_copy(tok[1][:, start:stop], tab[1][:].bitcast(U32).indirect(listed(start, stop)))
+        gates[2] = paged.tile([P, T], F32, name="gates2", offset=4 * T, align_bytes=64)
+        nc.sync.dma_start(gates[2][:], gT[2 * P : 3 * P, :])
+        for pair in range(3):
+            h_bf[pair] = held("h_bf%d" % pair, [P, 2 * K_PASS], BF16)
+        for jt in range(BANKS):
+            finish_tile(jt)
+            product(jt)
+        load_gates(3, "act0")
+        gather_gates(0, held("gated0", [P, J], F32, after="act2"))
+        finish_tile(4)
+        product(4)
+        quantise_h(0)
+        quantise_h(1)
+        finish_tile(5)
+        product(5)
+        gather_gates(1, held("gated1", [P, J], F32, after="act4"))
+        quantise_h(2)
+        finish_tile(6)
+        finish_tile(7)
         quantise_wd()
+        h_bf[3] = early.tile([P, 2 * K_PASS], BF16, name="h_bf3", offset=0, align_bytes=64)
+        product(6)
+        product(7)
         second_stage(0)
-        for jt in range(J_TILES // 2, J_TILES):
-            first_stage(jt)
+        gather_gates(2, held("gated2", [P, J], F32, after="act6"))
+        quantise_h(3)
         second_stage(1)
-        gather_gates(3, held("gated3", [P, J], F32, after="act%d" % (J_TILES - 1)))
-        for u in range(2):
-            scatter_half(0, u)
+        scatter(0, 0, HALF)
+        gather_gates(3, early.tile([P, J], F32, name="gated3", offset=0, align_bytes=64))
+        scatter(0, HALF, J)
         store(0)
         for n in range(1, N_TILES - 1):
-            scatter(n)
+            scatter(n, 0, J)
             store(n)
         last = N_TILES - 1
-        scatter(last)
+        scatter(last, 0, J)
         for queue, cols in ((nc.sync, slice(0, T // 2)), (nc.scalar, slice(T // 2, T))):
             queue.dma_start(out[P * last : P * (last + 1), cols], pages[last % PAGES][:, cols])

@@ -139,11 +139,22 @@ def tile_list_modp_ggelu_gate_kernel(
         ups = {}
         gas = {}
         acts = {}
+        lifted = {}
         gated = {}
-        h_bf = {}
+        late = ctx.enter_context(tc.tile_pool(name="late", bufs=1))
         h_codes = [held("h_codes%d" % u, [P, HALF], U32) for u in range(2)]
         h_plane = [held("h_plane%d" % u, [P, HALF], U8) for u in range(2)]
-        y = [held("y%d" % n, [P, J], F32) for n in range(N_TILES)]
+        y_half = {}
+        y_half[0, 0] = late.tile([P, HALF], F32, name="y00", offset=8 * HALF - 64, align_bytes=64)
+        y_half[1, 0] = held("y10", [P, HALF], F32)
+        y_half[0, 1] = held("y01", [P, HALF], F32)
+        y_half[1, 1] = held("y11", [P, HALF], F32)
+        y_whole = {n: held("y%d" % n, [P, J], F32) for n in range(PAGES, N_TILES)}
+
+        def y_part(n, u):
+            if n < PAGES:
+                return y_half[n, u][:]
+            return y_whole[n][:, HALF * u : HALF * (u + 1)]
 
         def first_pass(acc, jt, a, weights, planes):
             for s in range(PACK):
@@ -188,20 +199,16 @@ def tile_list_modp_ggelu_gate_kernel(
             if jt >= BANKS:
                 up_pass(jt, 0)
             up_pass(jt, 1)
+            if jt >= BANKS:
+                lifted[jt] = held("lifted%d" % jt, [P, P, PACK], F32)
+                nc.scalar.copy(lifted[jt][:], ups[jt][:].rearrange("p s j -> p j s"))
 
-        def product(jt):
-            pair, place = divmod(jt, 2)
-            nc.vector.tensor_tensor(
-                h_bf[pair][:, K_PASS * place : K_PASS * (place + 1)].rearrange("p (j s) -> p j s", s=PACK),
-                ups[jt][:].rearrange("p s j -> p j s"),
-                acts[jt][:],
-                MULT,
-            )
+        def h_slot(tile, jt):
+            place = jt % BANKS
+            return tile[:, K_PASS * place : K_PASS * (place + 1)].rearrange("p (j s) -> p j s", s=PACK)
 
-        def quantise_h(pair):
-            u, place = divmod(pair, 2)
-            cols = slice(2 * P * place, 2 * P * (place + 1))
-            nc.vector.quantize_mx(out=h_codes[u][:, cols].bitcast(FP8X4), scales=h_plane[u][:, cols], in_=h_bf[pair][:])
+        def quantise_h(u, tile):
+            nc.vector.quantize_mx(out=h_codes[u][:].bitcast(FP8X4), scales=h_plane[u][:], in_=tile[:])
 
         def gather_gates(n, tile):
             gated[n] = tile
@@ -211,30 +218,35 @@ def tile_list_modp_ggelu_gate_kernel(
         wd_plane = held("wd_plane", [P, N], U8)
         wd_bf = held("wd_bf", [P, PACK * N], BF16)
 
-        def quantise_wd():
+        def round_wd(u):
             dst = wd_bf[:].rearrange("p (u m c s) -> p u m s c", u=2, c=4, s=PACK)
             src = wd_raw[:].rearrange("p s (u m c) -> p u m s c", u=2, c=4)
-            for u in range(2):
-                nc.scalar.copy(dst[:, u], src[:, u])
-            nc.vector.quantize_mx(out=wd_codes[:].bitcast(FP8X4), scales=wd_plane[:], in_=wd_bf[:])
+            nc.scalar.copy(dst[:, u], src[:, u])
 
-        def second_stage(u):
-            for n in range(N_TILES):
-                acc = psum.tile([P, HALF], F32, name="acc", tag="gate")
-                nc.tensor.matmul_mx(
-                    out=acc[:],
-                    lhsT=wd_codes[:, P * n : P * (n + 1)].bitcast(FP8X4),
-                    lhsT_scale=wd_plane[:, P * n : P * (n + 1)],
-                    rhs=h_codes[u][:].bitcast(FP8X4),
-                    rhs_scale=h_plane[u][:],
-                    start=True,
-                    stop=True,
-                )
-                nc.scalar.copy(y[n][:, HALF * u : HALF * (u + 1)], acc[:])
+        def quantise_wd(u):
+            cols = slice(2 * P * u, 2 * P * (u + 1))
+            nc.vector.quantize_mx(
+                out=wd_codes[:, cols].bitcast(FP8X4),
+                scales=wd_plane[:, cols],
+                in_=wd_bf[:, 2 * K_PASS * u : 2 * K_PASS * (u + 1)],
+            )
 
-        def scatter(n, start, stop):
+        def second_stage(n, u):
+            acc = psum.tile([P, HALF], F32, name="acc", tag="gate")
+            nc.tensor.matmul_mx(
+                out=acc[:],
+                lhsT=wd_codes[:, P * n : P * (n + 1)].bitcast(FP8X4),
+                lhsT_scale=wd_plane[:, P * n : P * (n + 1)],
+                rhs=h_codes[u][:].bitcast(FP8X4),
+                rhs_scale=h_plane[u][:],
+                start=True,
+                stop=True,
+            )
+            nc.scalar.copy(y_part(n, u), acc[:])
+
+        def scatter(n, start, stop, values):
             nc.vector.tensor_tensor(
-                pages[n % PAGES][:].indirect(listed(start, stop)), y[n][:, start:stop], gated[n][:, start:stop], MULT
+                pages[n % PAGES][:].indirect(listed(start, stop)), values, gated[n][:, start:stop], MULT
             )
 
         def store(n):
@@ -248,39 +260,49 @@ def tile_list_modp_ggelu_gate_kernel(
             nc.vector.tensor_copy(tok[1][:, start:stop], tab[1][:].bitcast(U32).indirect(listed(start, stop)))
         gates[2] = paged.tile([P, T], F32, name="gates2", offset=4 * T, align_bytes=64)
         nc.sync.dma_start(gates[2][:], gT[2 * P : 3 * P, :])
-        for pair in range(3):
-            h_bf[pair] = held("h_bf%d" % pair, [P, 2 * K_PASS], BF16)
+
+        h_first = held("h_first", [P, BANKS * K_PASS], BF16)
         for jt in range(BANKS):
             finish_tile(jt)
-            product(jt)
+            nc.vector.tensor_tensor(
+                h_slot(h_first, jt), ups[jt][:].rearrange("p s j -> p j s"), acts[jt][:], MULT
+            )
         load_gates(3, "act0")
         gather_gates(0, held("gated0", [P, J], F32, after="act2"))
-        finish_tile(4)
-        product(4)
-        quantise_h(0)
-        quantise_h(1)
-        finish_tile(5)
-        product(5)
-        gather_gates(1, held("gated1", [P, J], F32, after="act4"))
-        quantise_h(2)
-        finish_tile(6)
-        finish_tile(7)
-        quantise_wd()
-        h_bf[3] = early.tile([P, 2 * K_PASS], BF16, name="h_bf3", offset=0, align_bytes=64)
-        product(6)
-        product(7)
-        second_stage(0)
-        gather_gates(2, held("gated2", [P, J], F32, after="act6"))
-        quantise_h(3)
-        second_stage(1)
-        scatter(0, 0, HALF)
-        gather_gates(3, early.tile([P, J], F32, name="gated3", offset=0, align_bytes=64))
-        scatter(0, HALF, J)
-        store(0)
-        for n in range(1, N_TILES - 1):
-            scatter(n, 0, J)
+        quantise_h(0, h_first)
+        round_wd(0)
+        round_wd(1)
+        quantise_wd(0)
+        gather_gates(1, held("gated1", [P, J], F32))
+        quantise_wd(1)
+        for n in range(PAGES):
+            second_stage(n, 0)
+        for jt in range(BANKS, J_TILES):
+            finish_tile(jt)
+        for n in range(PAGES, N_TILES):
+            second_stage(n, 0)
+
+        ready0 = held("ready0", [P, HALF], F32)
+        nc.vector.tensor_tensor(ready0[:], y_half[0, 0][:], gated[0][:, 0:HALF], MULT)
+        ready1 = late.tile([P, HALF], F32, name="ready1", offset=12 * HALF - 128, align_bytes=64)
+        nc.gpsimd.tensor_tensor(ready1[:], y_half[1, 0][:], gated[1][:, 0:HALF], MULT)
+        h_second = late.tile([P, BANKS * K_PASS], BF16, name="h_second", offset=0, align_bytes=64)
+        for jt in range(BANKS, J_TILES):
+            nc.gpsimd.tensor_tensor(h_slot(h_second, jt), lifted[jt][:], acts[jt][:], MULT)
+        for n, ready in enumerate((ready0, ready1)):
+            nc.vector.tensor_copy(pages[n][:].indirect(listed(0, HALF)), ready[:])
+
+        quantise_h(1, h_second)
+        gather_gates(2, held("gated2", [P, J], F32, after="lifted7"))
+        for n in range(N_TILES):
+            second_stage(n, 1)
+        for n in range(PAGES):
+            scatter(n, HALF, J, y_half[n, 1][:])
             store(n)
+        gather_gates(3, held("gated3", [P, J], F32, after="y01"))
+        scatter(2, 0, J, y_whole[2][:])
+        store(2)
         last = N_TILES - 1
-        scatter(last, 0, J)
+        scatter(last, 0, J, y_whole[last][:])
         for queue, cols in ((nc.sync, slice(0, T // 2)), (nc.scalar, slice(T // 2, T))):
             queue.dma_start(out[P * last : P * (last + 1), cols], pages[last % PAGES][:, cols])

@@ -26,6 +26,8 @@ J_TILES = J // P
 N_TILES = N // P
 PAGES = 2
 BANKS = 4
+WD_AT = 8192
+FACTORS_AT = WD_AT + 128
 
 
 def tile_list_modp_ggelu_gate_kernel(
@@ -36,6 +38,7 @@ def tile_list_modp_ggelu_gate_kernel(
         keep = ctx.enter_context(tc.tile_pool(name="keep", bufs=1))
         early = ctx.enter_context(tc.tile_pool(name="early", bufs=1))
         paged = ctx.enter_context(tc.tile_pool(name="paged", bufs=1))
+        late = ctx.enter_context(tc.tile_pool(name="late", bufs=1))
         psum = ctx.enter_context(tc.psum_pool(name="psum", bufs=BANKS))
 
         def held(name, shape, dtype, after=None):
@@ -106,13 +109,17 @@ def tile_list_modp_ggelu_gate_kernel(
         )
         router = held("router", [P, J], F32, after="wu_raw")
         nc.sync.dma_start(router[:], wgo)
+
         pages.append(paged.tile([P, T], F32, name="page1", offset=0, align_bytes=64))
         nc.vector.memset(pages[1][:].bitcast(I32), 0)
 
         wg_codes = [held("wg_codes%d" % a, [P, R], U32) for a in range(PASSES)]
         wg_plane = [held("wg_plane%d" % a, [P, R], U8) for a in range(PASSES)]
         for a in range(PASSES):
-            wg_bf = held("wg_bf%d" % a, [P, PACK * R], BF16)
+            if a == 0:
+                wg_bf = late.tile([P, PACK * R], BF16, name="wg_bf0", offset=WD_AT, align_bytes=64)
+            else:
+                wg_bf = held("wg_bf1", [P, PACK * R], BF16)
             dst = wg_bf[:].rearrange("p (s g u c i) -> p s g u i c", s=PACK, u=2, c=4, i=PACK)
             src = wg_raw[a][:].rearrange("p i (g s u c) -> p s g u i c", s=PACK, u=2, c=4)
             for s in range(PACK):
@@ -129,7 +136,7 @@ def tile_list_modp_ggelu_gate_kernel(
                 )
 
         load_gates(0, "wg_raw0")
-        wd_raw = held("wd_raw", [P, PACK, N], F32, after="wg_bf0")
+        wd_raw = late.tile([P, PACK, N], F32, name="wd_raw", offset=WD_AT, align_bytes=64)
         wd_rows = wd.rearrange("(g s q) n -> s g q n", s=PACK, q=8)
         for s in range(PACK):
             nc.sync.dma_start(wd_raw[:, s, :], wd_rows[s])
@@ -140,12 +147,12 @@ def tile_list_modp_ggelu_gate_kernel(
         gas = {}
         acts = {}
         lifted = {}
+        factors = []
         gated = {}
-        late = ctx.enter_context(tc.tile_pool(name="late", bufs=1))
         h_codes = [held("h_codes%d" % u, [P, HALF], U32) for u in range(2)]
-        h_plane = [held("h_plane%d" % u, [P, HALF], U8) for u in range(2)]
+        h_plane = [held("h_plane0", [P, HALF], U8)]
         y_half = {}
-        y_half[0, 0] = late.tile([P, HALF], F32, name="y00", offset=8 * HALF - 64, align_bytes=64)
+        y_half[0, 0] = held("y00", [P, HALF], F32)
         y_half[1, 0] = held("y10", [P, HALF], F32)
         y_half[0, 1] = held("y01", [P, HALF], F32)
         y_half[1, 1] = held("y11", [P, HALF], F32)
@@ -194,14 +201,19 @@ def tile_list_modp_ggelu_gate_kernel(
             if jt >= BANKS:
                 gate_pass(jt, 0)
             gate_pass(jt, 1)
-            acts[jt] = held("act%d" % jt, [P, P, PACK], F32)
-            nc.scalar.activation(acts[jt][:], gas[jt][:].rearrange("p s j -> p j s"), GELU)
+            if jt < BANKS:
+                acts[jt] = held("act%d" % jt, [P, P, PACK], F32)[:]
+            elif jt == BANKS:
+                acts[jt] = late.tile([P, P, PACK], F32, name="act4", offset=WD_AT - 4 * HALF + 64, align_bytes=64)[:]
+            else:
+                acts[jt] = factors[0][:, 0, jt - BANKS]
+            nc.scalar.activation(acts[jt], gas[jt][:].rearrange("p s j -> p j s"), GELU)
             if jt >= BANKS:
                 up_pass(jt, 0)
             up_pass(jt, 1)
-            if jt >= BANKS:
-                lifted[jt] = held("lifted%d" % jt, [P, P, PACK], F32)
-                nc.scalar.copy(lifted[jt][:], ups[jt][:].rearrange("p s j -> p j s"))
+            if jt > BANKS:
+                lifted[jt] = factors[0][:, 1, jt - BANKS]
+                nc.scalar.copy(lifted[jt], ups[jt][:].rearrange("p s j -> p j s"))
 
         def h_slot(tile, jt):
             place = jt % BANKS
@@ -265,7 +277,7 @@ def tile_list_modp_ggelu_gate_kernel(
         for jt in range(BANKS):
             finish_tile(jt)
             nc.vector.tensor_tensor(
-                h_slot(h_first, jt), ups[jt][:].rearrange("p s j -> p j s"), acts[jt][:], MULT
+                h_slot(h_first, jt), ups[jt][:].rearrange("p s j -> p j s"), acts[jt], MULT
             )
         load_gates(3, "act0")
         gather_gates(0, held("gated0", [P, J], F32, after="act2"))
@@ -277,6 +289,7 @@ def tile_list_modp_ggelu_gate_kernel(
         quantise_wd(1)
         for n in range(PAGES):
             second_stage(n, 0)
+        factors.append(late.tile([P, 2, BANKS, P, PACK], F32, name="factors", offset=FACTORS_AT, align_bytes=64))
         for jt in range(BANKS, J_TILES):
             finish_tile(jt)
         for n in range(PAGES, N_TILES):
@@ -284,16 +297,24 @@ def tile_list_modp_ggelu_gate_kernel(
 
         ready0 = held("ready0", [P, HALF], F32)
         nc.vector.tensor_tensor(ready0[:], y_half[0, 0][:], gated[0][:, 0:HALF], MULT)
-        ready1 = late.tile([P, HALF], F32, name="ready1", offset=12 * HALF - 128, align_bytes=64)
-        nc.gpsimd.tensor_tensor(ready1[:], y_half[1, 0][:], gated[1][:, 0:HALF], MULT)
-        h_second = late.tile([P, BANKS * K_PASS], BF16, name="h_second", offset=0, align_bytes=64)
-        for jt in range(BANKS, J_TILES):
-            nc.gpsimd.tensor_tensor(h_slot(h_second, jt), lifted[jt][:], acts[jt][:], MULT)
+        h_fifth = held("h_fifth", [P, K_PASS], BF16, after="wd_bf")
+        nc.vector.tensor_tensor(
+            h_slot(h_fifth, BANKS), ups[BANKS][:].rearrange("p s j -> p j s"), acts[BANKS], MULT
+        )
+        ready1 = late.tile([P, HALF], F32, name="ready1", offset=FACTORS_AT - 4 * HALF, align_bytes=64)
+        for cols in (slice(0, 2 * P), slice(2 * P, HALF)):
+            nc.gpsimd.tensor_tensor(ready1[:, cols], y_half[1, 0][:, cols], gated[1][:, cols], MULT)
+        h_rest = late.tile([P, (BANKS - 1) * K_PASS], BF16, name="h_rest", offset=FACTORS_AT - 10 * HALF, align_bytes=64)
+        for jt in range(BANKS + 1, J_TILES):
+            for rows in (slice(0, P // 2), slice(P // 2, P)):
+                nc.gpsimd.tensor_tensor(h_slot(h_rest, jt - 1)[:, rows], lifted[jt][:, rows], acts[jt][:, rows], MULT)
         for n, ready in enumerate((ready0, ready1)):
             nc.vector.tensor_copy(pages[n][:].indirect(listed(0, HALF)), ready[:])
 
-        quantise_h(1, h_second)
-        gather_gates(2, held("gated2", [P, J], F32, after="lifted7"))
+        h_plane.append(late.tile([P, HALF], U8, name="h_plane1", offset=FACTORS_AT, align_bytes=64))
+        for tile, cols in ((h_fifth, slice(0, P)), (h_rest, slice(P, HALF))):
+            nc.vector.quantize_mx(out=h_codes[1][:, cols].bitcast(FP8X4), scales=h_plane[1][:, cols], in_=tile[:])
+        gather_gates(2, late.tile([P, J], F32, name="gated2", offset=FACTORS_AT + HALF, align_bytes=64))
         for n in range(N_TILES):
             second_stage(n, 1)
         for n in range(PAGES):

@@ -26,7 +26,7 @@ J_TILES = J // P
 N_TILES = N // P
 PAGES = 2
 BANKS = 4
-WD_AT = 8192
+WD_AT = 10240
 FACTORS_AT = WD_AT + 128
 
 
@@ -136,10 +136,15 @@ def tile_list_modp_ggelu_gate_kernel(
                 )
 
         load_gates(0, "wg_raw0")
-        wd_raw = late.tile([P, PACK, N], F32, name="wd_raw", offset=WD_AT, align_bytes=64)
+        wd_raw = {}
         wd_rows = wd.rearrange("(g s q) n -> s g q n", s=PACK, q=8)
-        for s in range(PACK):
-            nc.sync.dma_start(wd_raw[:, s, :], wd_rows[s])
+
+        def load_wd(u, tile):
+            wd_raw[u] = tile
+            for s in range(PACK):
+                nc.sync.dma_start(tile[:, s, :], wd_rows[s, :, :, N // 2 * u : N // 2 * (u + 1)])
+
+        load_wd(0, late.tile([P, PACK, N // 2], F32, name="wd_raw0", offset=WD_AT, align_bytes=64))
         gates[1] = early.tile([P, T], F32, name="gates1", offset=0, align_bytes=64)
         nc.sync.dma_start(gates[1][:], gT[P : 2 * P, :])
 
@@ -152,7 +157,7 @@ def tile_list_modp_ggelu_gate_kernel(
         h_codes = [held("h_codes%d" % u, [P, HALF], U32) for u in range(2)]
         h_plane = [held("h_plane0", [P, HALF], U8)]
         y_half = {}
-        y_half[0, 0] = held("y00", [P, HALF], F32)
+        y_half[0, 0] = late.tile([P, HALF], F32, name="y00", offset=6 * HALF - 64, align_bytes=64)
         y_half[1, 0] = held("y10", [P, HALF], F32)
         y_half[0, 1] = held("y01", [P, HALF], F32)
         y_half[1, 1] = held("y11", [P, HALF], F32)
@@ -227,19 +232,18 @@ def tile_list_modp_ggelu_gate_kernel(
             nc.vector.tensor_tensor(gated[n][:], gates[n][:].indirect(offsets[:]), router[:], MULT)
 
         wd_codes = held("wd_codes", [P, N], U32)
-        wd_plane = held("wd_plane", [P, N], U8)
+        wd_plane = [held("wd_plane0", [P, N // 2], U8)]
         wd_bf = held("wd_bf", [P, PACK * N], BF16)
 
         def round_wd(u):
             dst = wd_bf[:].rearrange("p (u m c s) -> p u m s c", u=2, c=4, s=PACK)
-            src = wd_raw[:].rearrange("p s (u m c) -> p u m s c", u=2, c=4)
-            nc.scalar.copy(dst[:, u], src[:, u])
+            nc.scalar.copy(dst[:, u], wd_raw[u][:].rearrange("p s (m c) -> p m s c", c=4))
 
         def quantise_wd(u):
             cols = slice(2 * P * u, 2 * P * (u + 1))
             nc.vector.quantize_mx(
                 out=wd_codes[:, cols].bitcast(FP8X4),
-                scales=wd_plane[:, cols],
+                scales=wd_plane[u][:],
                 in_=wd_bf[:, 2 * K_PASS * u : 2 * K_PASS * (u + 1)],
             )
 
@@ -248,7 +252,7 @@ def tile_list_modp_ggelu_gate_kernel(
             nc.tensor.matmul_mx(
                 out=acc[:],
                 lhsT=wd_codes[:, P * n : P * (n + 1)].bitcast(FP8X4),
-                lhsT_scale=wd_plane[:, P * n : P * (n + 1)],
+                lhsT_scale=wd_plane[n // 2][:, P * (n % 2) : P * (n % 2 + 1)],
                 rhs=h_codes[u][:].bitcast(FP8X4),
                 rhs_scale=h_plane[u][:],
                 start=True,
@@ -279,44 +283,46 @@ def tile_list_modp_ggelu_gate_kernel(
             nc.vector.tensor_tensor(
                 h_slot(h_first, jt), ups[jt][:].rearrange("p s j -> p j s"), acts[jt], MULT
             )
-        load_gates(3, "act0")
+        load_wd(1, held("wd_raw1", [P, PACK, N // 2], F32, after="act0"))
+        load_gates(3, "act1")
         gather_gates(0, held("gated0", [P, J], F32, after="act2"))
         quantise_h(0, h_first)
         round_wd(0)
-        round_wd(1)
         quantise_wd(0)
         gather_gates(1, held("gated1", [P, J], F32))
-        quantise_wd(1)
+        factors.append(late.tile([P, 2, BANKS, P, PACK], F32, name="factors", offset=FACTORS_AT, align_bytes=64))
+        for jt in range(BANKS, J_TILES - 1):
+            finish_tile(jt)
         for n in range(PAGES):
             second_stage(n, 0)
-        factors.append(late.tile([P, 2, BANKS, P, PACK], F32, name="factors", offset=FACTORS_AT, align_bytes=64))
-        for jt in range(BANKS, J_TILES):
-            finish_tile(jt)
-        for n in range(PAGES, N_TILES):
-            second_stage(n, 0)
+        finish_tile(J_TILES - 1)
+        round_wd(1)
 
         ready0 = held("ready0", [P, HALF], F32)
         nc.vector.tensor_tensor(ready0[:], y_half[0, 0][:], gated[0][:, 0:HALF], MULT)
-        h_fifth = held("h_fifth", [P, K_PASS], BF16, after="wd_bf")
+        h_fifth = held("h_fifth", [P, K_PASS], BF16)
         nc.vector.tensor_tensor(
             h_slot(h_fifth, BANKS), ups[BANKS][:].rearrange("p s j -> p j s"), acts[BANKS], MULT
         )
-        ready1 = late.tile([P, HALF], F32, name="ready1", offset=FACTORS_AT - 4 * HALF, align_bytes=64)
-        for cols in (slice(0, 2 * P), slice(2 * P, HALF)):
-            nc.gpsimd.tensor_tensor(ready1[:, cols], y_half[1, 0][:, cols], gated[1][:, cols], MULT)
-        h_rest = late.tile([P, (BANKS - 1) * K_PASS], BF16, name="h_rest", offset=FACTORS_AT - 10 * HALF, align_bytes=64)
-        for jt in range(BANKS + 1, J_TILES):
-            for rows in (slice(0, P // 2), slice(P // 2, P)):
-                nc.gpsimd.tensor_tensor(h_slot(h_rest, jt - 1)[:, rows], lifted[jt][:, rows], acts[jt][:, rows], MULT)
+        ready1 = late.tile([P, HALF], F32, name="ready1", offset=10 * HALF - 128, align_bytes=64)
+        nc.gpsimd.tensor_tensor(ready1[:], y_half[1, 0][:], gated[1][:, 0:HALF], MULT)
+        h_rest = late.tile([P, (BANKS - 1) * K_PASS], BF16, name="h_rest", offset=0, align_bytes=64)
+        rest = factors[0][:, :, 1:BANKS].rearrange("p f t j s -> p f (t j s)")
+        nc.gpsimd.tensor_tensor(h_rest[:], rest[:, 1], rest[:, 0], MULT)
         for n, ready in enumerate((ready0, ready1)):
             nc.vector.tensor_copy(pages[n][:].indirect(listed(0, HALF)), ready[:])
 
         h_plane.append(late.tile([P, HALF], U8, name="h_plane1", offset=FACTORS_AT, align_bytes=64))
         for tile, cols in ((h_fifth, slice(0, P)), (h_rest, slice(P, HALF))):
             nc.vector.quantize_mx(out=h_codes[1][:, cols].bitcast(FP8X4), scales=h_plane[1][:, cols], in_=tile[:])
+        wd_plane.append(late.tile([P, N // 2], U8, name="wd_plane1", offset=FACTORS_AT + HALF + 4 * J, align_bytes=64))
+        quantise_wd(1)
         gather_gates(2, late.tile([P, J], F32, name="gated2", offset=FACTORS_AT + HALF, align_bytes=64))
-        for n in range(N_TILES):
+        for n in range(PAGES):
             second_stage(n, 1)
+        for n in range(PAGES, N_TILES):
+            for u in range(2):
+                second_stage(n, u)
         for n in range(PAGES):
             scatter(n, HALF, J, y_half[n, 1][:])
             store(n)

@@ -155,9 +155,9 @@ def tile_list_modp_ggelu_gate_kernel(
         factors = []
         gated = {}
         h_codes = [held("h_codes%d" % u, [P, HALF], U32) for u in range(2)]
-        h_plane = [held("h_plane0", [P, HALF], U8)]
+        h_plane = [held("h_plane%d" % u, [P, HALF], U8) for u in range(2)]
         y_half = {}
-        y_half[0, 0] = late.tile([P, HALF], F32, name="y00", offset=6 * HALF - 64, align_bytes=64)
+        y_half[0, 0] = late.tile([P, HALF], F32, name="y00", offset=8 * HALF - 64, align_bytes=64)
         y_half[1, 0] = held("y10", [P, HALF], F32)
         y_half[0, 1] = held("y01", [P, HALF], F32)
         y_half[1, 1] = held("y11", [P, HALF], F32)
@@ -208,15 +208,13 @@ def tile_list_modp_ggelu_gate_kernel(
             gate_pass(jt, 1)
             if jt < BANKS:
                 acts[jt] = held("act%d" % jt, [P, P, PACK], F32)[:]
-            elif jt == BANKS:
-                acts[jt] = late.tile([P, P, PACK], F32, name="act4", offset=WD_AT - 4 * HALF + 64, align_bytes=64)[:]
             else:
                 acts[jt] = factors[0][:, 0, jt - BANKS]
             nc.scalar.activation(acts[jt], gas[jt][:].rearrange("p s j -> p j s"), GELU)
             if jt >= BANKS:
                 up_pass(jt, 0)
             up_pass(jt, 1)
-            if jt > BANKS:
+            if jt >= BANKS:
                 lifted[jt] = factors[0][:, 1, jt - BANKS]
                 nc.scalar.copy(lifted[jt], ups[jt][:].rearrange("p s j -> p j s"))
 
@@ -300,21 +298,15 @@ def tile_list_modp_ggelu_gate_kernel(
 
         ready0 = held("ready0", [P, HALF], F32)
         nc.vector.tensor_tensor(ready0[:], y_half[0, 0][:], gated[0][:, 0:HALF], MULT)
-        h_fifth = held("h_fifth", [P, K_PASS], BF16)
-        nc.vector.tensor_tensor(
-            h_slot(h_fifth, BANKS), ups[BANKS][:].rearrange("p s j -> p j s"), acts[BANKS], MULT
-        )
-        ready1 = late.tile([P, HALF], F32, name="ready1", offset=10 * HALF - 128, align_bytes=64)
+        ready1 = late.tile([P, HALF], F32, name="ready1", offset=12 * HALF - 128, align_bytes=64)
         nc.gpsimd.tensor_tensor(ready1[:], y_half[1, 0][:], gated[1][:, 0:HALF], MULT)
-        h_rest = late.tile([P, (BANKS - 1) * K_PASS], BF16, name="h_rest", offset=0, align_bytes=64)
-        rest = factors[0][:, :, 1:BANKS].rearrange("p f t j s -> p f (t j s)")
-        nc.gpsimd.tensor_tensor(h_rest[:], rest[:, 1], rest[:, 0], MULT)
+        h_second = late.tile([P, BANKS * K_PASS], BF16, name="h_second", offset=0, align_bytes=64)
+        both = factors[0][:].rearrange("p f t j s -> p f (t j s)")
+        nc.gpsimd.tensor_tensor(h_second[:], both[:, 1], both[:, 0], MULT)
         for n, ready in enumerate((ready0, ready1)):
             nc.vector.tensor_copy(pages[n][:].indirect(listed(0, HALF)), ready[:])
 
-        h_plane.append(late.tile([P, HALF], U8, name="h_plane1", offset=FACTORS_AT, align_bytes=64))
-        for tile, cols in ((h_fifth, slice(0, P)), (h_rest, slice(P, HALF))):
-            nc.vector.quantize_mx(out=h_codes[1][:, cols].bitcast(FP8X4), scales=h_plane[1][:, cols], in_=tile[:])
+        quantise_h(1, h_second)
         wd_plane.append(late.tile([P, N // 2], U8, name="wd_plane1", offset=FACTORS_AT + HALF + 4 * J, align_bytes=64))
         quantise_wd(1)
         gather_gates(2, late.tile([P, J], F32, name="gated2", offset=FACTORS_AT + HALF, align_bytes=64))

@@ -1,6 +1,7 @@
 from contextlib import ExitStack
 
 import concourse.mybir as mybir
+from concourse.masks import make_identity
 
 K, R, N, T, J = 1024, 512, 512, 2048, 1024
 FLOPS = 2 * J * (2 * K * R + R * N)
@@ -60,6 +61,10 @@ def tile_list_modp_ggelu_gate_kernel(
         pages = [held("page0", [P, T], F32)]
         nc.vector.memset(pages[0][:].bitcast(I32), 0)
 
+        identity = held("identity", [P, P], F32)
+        nc.vector.memset(identity[:], 0.0)
+        make_identity(nc, identity[:], nomemset=True)
+
         tab = {}
         gates = {}
         wg_raw = {}
@@ -77,6 +82,8 @@ def tile_list_modp_ggelu_gate_kernel(
             nc.sync.dma_start(tile[:], wg[K_PASS * a : K_PASS * (a + 1), :].rearrange("(p i) r -> p i r", i=PACK))
 
         nc.sync.dma_start(tab_rows[96:128, :].bitcast(I32), tab_scales.bitcast(I32).rearrange("a b w -> b a w"))
+        weight_runs = held("weight_runs", [P, J // P], F32)
+        nc.sync.dma_start(weight_runs[:], wgo[0].rearrange("(q m) -> q m", m=J // P))
         for q in range(QUADS):
             nc.scalar.dma_start(
                 wu_planes_raw[32 * q : 32 * q + 4],
@@ -86,6 +93,15 @@ def tile_list_modp_ggelu_gate_kernel(
         wu_raw = held("wu_raw", [P, PASSES, R // 2], I32)
         nc.sync.dma_start(wu_raw[:], wu_words.bitcast(I32).rearrange("a p w -> p a w"))
         load_wg(0, held("wg_raw0", [P, PACK, R], F32))
+
+        router = held("router", [P, J], F32)
+        router_runs = router[:].rearrange("p (q m) -> p q m", m=J // P)
+        for half in range(2):
+            spread = psum.tile([P, PACK, P], F32, name="spread", tag="gate")
+            for m in range(PACK):
+                column = PACK * half + m
+                nc.tensor.transpose(spread[:, m, :], weight_runs[:, column : column + 1].to_broadcast([P, P]), identity[:])
+            nc.scalar.copy(router_runs[:, :, PACK * half : PACK * (half + 1)], spread[:].rearrange("p m q -> p q m"))
 
         tok = [held("tok%d" % a, [P, J], U32) for a in range(PASSES)]
         tok_rows = held("tok_rows", [P, J], U8)
@@ -107,8 +123,6 @@ def tile_list_modp_ggelu_gate_kernel(
             wu[:].bitcast(I32).rearrange("p a (s g w) -> p a s g w", s=PACK, w=4),
             wu_raw[:].rearrange("p a (g s w) -> p a s g w", s=PACK, w=4),
         )
-        router = held("router", [P, J], F32, after="wu_raw")
-        nc.sync.dma_start(router[:], wgo)
 
         pages.append(paged.tile([P, T], F32, name="page1", offset=0, align_bytes=64))
         nc.vector.memset(pages[1][:].bitcast(I32), 0)
@@ -155,7 +169,10 @@ def tile_list_modp_ggelu_gate_kernel(
         factors = []
         gated = {}
         h_codes = [held("h_codes%d" % u, [P, HALF], U32) for u in range(2)]
-        h_plane = [held("h_plane%d" % u, [P, HALF], U8) for u in range(2)]
+        h_plane = [
+            late.tile([P, HALF], U8, name="h_plane0", offset=WD_AT - HALF + 64, align_bytes=64),
+            held("h_plane1", [P, HALF], U8),
+        ]
         y_half = {}
         y_half[0, 0] = late.tile([P, HALF], F32, name="y00", offset=8 * HALF - 64, align_bytes=64)
         y_half[1, 0] = held("y10", [P, HALF], F32)
@@ -231,18 +248,18 @@ def tile_list_modp_ggelu_gate_kernel(
 
         wd_codes = held("wd_codes", [P, N], U32)
         wd_plane = [held("wd_plane0", [P, N // 2], U8)]
-        wd_bf = held("wd_bf", [P, PACK * N], BF16)
+        wd_bf = [held("wd_bf%d" % u, [P, PACK * N // 2], BF16) for u in range(2)]
 
         def round_wd(u):
-            dst = wd_bf[:].rearrange("p (u m c s) -> p u m s c", u=2, c=4, s=PACK)
-            nc.scalar.copy(dst[:, u], wd_raw[u][:].rearrange("p s (m c) -> p m s c", c=4))
+            dst = wd_bf[u][:].rearrange("p (m c s) -> p m s c", c=4, s=PACK)
+            nc.scalar.copy(dst, wd_raw[u][:].rearrange("p s (m c) -> p m s c", c=4))
 
         def quantise_wd(u):
             cols = slice(2 * P * u, 2 * P * (u + 1))
             nc.vector.quantize_mx(
                 out=wd_codes[:, cols].bitcast(FP8X4),
                 scales=wd_plane[u][:],
-                in_=wd_bf[:, 2 * K_PASS * u : 2 * K_PASS * (u + 1)],
+                in_=wd_bf[u][:],
             )
 
         def second_stage(n, u):
@@ -281,13 +298,14 @@ def tile_list_modp_ggelu_gate_kernel(
             nc.vector.tensor_tensor(
                 h_slot(h_first, jt), ups[jt][:].rearrange("p s j -> p j s"), acts[jt], MULT
             )
+            if jt == 1:
+                gather_gates(0, held("gated0", [P, J], F32))
         load_wd(1, held("wd_raw1", [P, PACK, N // 2], F32, after="act0"))
         load_gates(3, "act1")
-        gather_gates(0, held("gated0", [P, J], F32, after="act2"))
-        quantise_h(0, h_first)
         round_wd(0)
         quantise_wd(0)
-        gather_gates(1, held("gated1", [P, J], F32))
+        quantise_h(0, h_first)
+        gather_gates(1, held("gated1", [P, J], F32, after="wd_bf0"))
         factors.append(late.tile([P, 2, BANKS, P, PACK], F32, name="factors", offset=FACTORS_AT, align_bytes=64))
         for jt in range(BANKS, J_TILES - 1):
             finish_tile(jt)

@@ -54,23 +54,22 @@ def tile_list_modp_ggelu_gate_kernel(
         tab_rows = early.tile([P, T], U8, name="tab_rows", offset=4 * T - T // 2, align_bytes=64)
         tok_planes = held("tok_planes", [P, PASSES * J], U8)
         wu_planes = held("wu_planes", [P, PASSES * R], U8)
-        wu_planes_raw = held("wu_planes_raw", [P, PASSES, R // 4], I32)
-        nc.vector.memset(wu_planes_raw[:], 0)
+        wu_rows = held("wu_rows", [P, PASSES, QUADS, R // 4], I32)
         nc.vector.memset(tab_rows[0:96, :].bitcast(I32), 0)
-        nc.vector.memset(tok_planes[:].bitcast(I32), 0)
-        pages = [held("page0", [P, T], F32)]
-        nc.vector.memset(pages[0][:].bitcast(I32), 0)
-
         identity = held("identity", [P, P], F32)
         nc.vector.memset(identity[:], 0.0)
         make_identity(nc, identity[:], nomemset=True)
+        nc.vector.memset(wu_planes[:].bitcast(I32), 0)
+        nc.vector.memset(tok_planes[:].bitcast(I32), 0)
+        pages = [held("page0", [P, T], F32)]
+        nc.vector.memset(pages[0][:].bitcast(I32), 0)
 
         tab = {}
         gates = {}
         wg_raw = {}
 
-        def load_tab(a):
-            tab[a] = paged.tile([P, T], I32, name="tab%d" % a, offset=2 * T * (a + 1), align_bytes=64)
+        def load_tab(a, tile):
+            tab[a] = tile
             nc.sync.dma_start(tab[a][:], tab_words[a].rearrange("p t i -> p (t i)").bitcast(I32))
 
         def load_gates(n, after):
@@ -84,12 +83,11 @@ def tile_list_modp_ggelu_gate_kernel(
         nc.sync.dma_start(tab_rows[96:128, :].bitcast(I32), tab_scales.bitcast(I32).rearrange("a b w -> b a w"))
         weight_runs = held("weight_runs", [P, J // P], F32)
         nc.sync.dma_start(weight_runs[:], wgo[0].rearrange("(q m) -> q m", m=J // P))
-        for q in range(QUADS):
-            nc.scalar.dma_start(
-                wu_planes_raw[32 * q : 32 * q + 4],
-                wu_scales[:, 4 * q : 4 * q + 4, :].bitcast(I32).rearrange("a p w -> p a w"),
-            )
-        load_tab(0)
+        nc.sync.dma_start(
+            wu_rows[0:4].rearrange("e a q w -> e (a q) w"),
+            wu_scales.bitcast(I32).rearrange("a (q e) w -> e (a q) w", e=4),
+        )
+        load_tab(0, paged.tile([P, T], I32, name="tab0", offset=0, align_bytes=64))
         wu_raw = held("wu_raw", [P, PASSES, R // 2], I32)
         nc.sync.dma_start(wu_raw[:], wu_words.bitcast(I32).rearrange("a p w -> p a w"))
         load_wg(0, held("wg_raw0", [P, PACK, R], F32))
@@ -111,18 +109,24 @@ def tile_list_modp_ggelu_gate_kernel(
                 tok_planes[32 * q : 32 * q + 4, :].bitcast(I32), tok_rows[96 + 8 * q : 96 + 8 * q + 8, :].bitcast(I32)
             )
         load_wg(1, early.tile([P, PACK, R], F32, name="wg_raw1", offset=0, align_bytes=64))
-        nc.vector.tensor_copy(tok[0][:], tab[0][:].bitcast(U32).indirect(offsets[:]))
-        load_tab(1)
+        load_tab(1, early.tile([P, T], I32, name="tab1", offset=4 * T, align_bytes=64))
 
-        nc.vector.tensor_copy(
-            wu_planes[:].bitcast(I32).rearrange("p (a s g w) -> p a s g w", a=PASSES, s=PACK, w=2),
-            wu_planes_raw[:].rearrange("p a (g s w) -> p a s g w", s=PACK, w=2),
-        )
+        planes_by_slot = wu_planes[:].bitcast(I32).rearrange("p (a s g w) -> p a s g w", a=PASSES, s=PACK, w=2)
+        for q in range(QUADS):
+            nc.vector.tensor_copy(
+                planes_by_slot[32 * q : 32 * q + 4],
+                wu_rows[0:4, :, q, :].rearrange("p a (g s w) -> p a s g w", s=PACK, w=2),
+            )
         wu = held("wu", [P, PASSES, 2 * R], U8)
-        nc.vector.tensor_copy(
-            wu[:].bitcast(I32).rearrange("p a (s g w) -> p a s g w", s=PACK, w=4),
-            wu_raw[:].rearrange("p a (g s w) -> p a s g w", s=PACK, w=4),
+        nc.scalar.copy(
+            wu[:].bitcast(U32).rearrange("p a (s g w) -> p a s g w", s=PACK, w=4),
+            wu_raw[:].bitcast(U32).rearrange("p a (g s w) -> p a s g w", s=PACK, w=4),
         )
+
+        for start in (0, HALF):
+            nc.vector.tensor_copy(
+                tok[0][:, start : start + HALF], tab[0][:].bitcast(U32).indirect(listed(start, start + HALF))
+            )
 
         pages.append(paged.tile([P, T], F32, name="page1", offset=0, align_bytes=64))
         nc.vector.memset(pages[1][:].bitcast(I32), 0)
@@ -289,7 +293,7 @@ def tile_list_modp_ggelu_gate_kernel(
             gate_pass(jt, 0)
         for start, stop in ((0, 2 * P), (2 * P, HALF), (HALF, J)):
             nc.vector.tensor_copy(tok[1][:, start:stop], tab[1][:].bitcast(U32).indirect(listed(start, stop)))
-        gates[2] = paged.tile([P, T], F32, name="gates2", offset=4 * T, align_bytes=64)
+        gates[2] = early.tile([P, T], F32, name="gates2", offset=4 * T, align_bytes=64)
         nc.sync.dma_start(gates[2][:], gT[2 * P : 3 * P, :])
 
         h_first = held("h_first", [P, BANKS * K_PASS], BF16)

from contextlib import ExitStack

import concourse.mybir as mybir
from concourse.masks import make_identity

K, R, N, T, J = 1024, 512, 512, 2048, 1024
FLOPS = 2 * J * (2 * K * R + R * N)

F32 = mybir.dt.float32
BF16 = mybir.dt.bfloat16
I32 = mybir.dt.int32
U32 = mybir.dt.uint32
U16 = mybir.dt.uint16
U8 = mybir.dt.uint8
FP8X4 = mybir.dt.float8_e4m3fn_x4
FP4X4 = mybir.dt.float4_e2m1fn_x4
MULT = mybir.AluOpType.mult
GELU = mybir.ActivationFunctionType.Gelu_apprx_tanh

P = 128
PACK = 4
K_PASS = P * PACK
PASSES = K // K_PASS
QUADS = 4
HALF = J // 2
J_TILES = J // P
N_TILES = N // P
PAGES = 2
BANKS = 4
WD_AT = 10240
FACTORS_AT = WD_AT + 128


def tile_list_modp_ggelu_gate_kernel(
    tc, tab_words, tab_scales, wg, wu_words, wu_scales, wd, gT, wgo, offs, out
):
    nc = tc.nc
    with ExitStack() as ctx:
        keep = ctx.enter_context(tc.tile_pool(name="keep", bufs=1))
        early = ctx.enter_context(tc.tile_pool(name="early", bufs=1))
        paged = ctx.enter_context(tc.tile_pool(name="paged", bufs=1))
        late = ctx.enter_context(tc.tile_pool(name="late", bufs=1))
        psum = ctx.enter_context(tc.psum_pool(name="psum", bufs=BANKS))

        def held(name, shape, dtype, after=None):
            return keep.tile(shape, dtype, name=name, tag=after or name, align_bytes=64)

        offsets = keep.tile([P, J // 16], U16, name="offsets")
        nc.sync.dma_start(offsets[:], offs)

        def listed(start, stop):
            return offsets[:, start // 16 : stop // 16]

        tab_rows = early.tile([P, T], U8, name="tab_rows", offset=4 * T - T // 2, align_bytes=64)
        tok_planes = held("tok_planes", [P, PASSES * J], U8)
        wu_planes = held("wu_planes", [P, PASSES * R], U8)
        wu_rows = held("wu_rows", [P, PASSES, QUADS, R // 4], I32)
        nc.vector.memset(tab_rows[0:96, :].bitcast(I32), 0)
        identity = held("identity", [P, P], F32)
        nc.vector.memset(identity[:], 0.0)
        make_identity(nc, identity[:], nomemset=True)
        nc.vector.memset(wu_planes[:].bitcast(I32), 0)
        nc.vector.memset(tok_planes[:].bitcast(I32), 0)
        pages = [held("page0", [P, T], F32)]
        nc.vector.memset(pages[0][:].bitcast(I32), 0)

        tab = {}
        gates = {}
        wg_raw = {}

        def load_tab(a, tile):
            tab[a] = tile
            nc.sync.dma_start(tab[a][:], tab_words[a].rearrange("p t i -> p (t i)").bitcast(I32))

        def load_gates(n, after):
            gates[n] = held("gates%d" % n, [P, T], F32, after=after)
            nc.sync.dma_start(gates[n][:], gT[P * n : P * (n + 1), :])

        def load_wg(a, tile):
            wg_raw[a] = tile
            nc.sync.dma_start(tile[:], wg[K_PASS * a : K_PASS * (a + 1), :].rearrange("(p i) r -> p i r", i=PACK))

        nc.sync.dma_start(tab_rows[96:128, :].bitcast(I32), tab_scales.bitcast(I32).rearrange("a b w -> b a w"))
        weight_runs = held("weight_runs", [P, J // P], F32)
        nc.sync.dma_start(weight_runs[:], wgo[0].rearrange("(q m) -> q m", m=J // P))
        nc.sync.dma_start(
            wu_rows[0:4].rearrange("e a q w -> e (a q) w"),
            wu_scales.bitcast(I32).rearrange("a (q e) w -> e (a q) w", e=4),
        )
        load_tab(0, paged.tile([P, T], I32, name="tab0", offset=0, align_bytes=64))
        wu_raw = held("wu_raw", [P, PASSES, R // 2], I32)
        nc.sync.dma_start(wu_raw[:], wu_words.bitcast(I32).rearrange("a p w -> p a w"))
        load_wg(0, held("wg_raw0", [P, PACK, R], F32))

        router = held("router", [P, J], F32)
        router_runs = router[:].rearrange("p (q m) -> p q m", m=J // P)
        for half in range(2):
            spread = psum.tile([P, PACK, P], F32, name="spread", tag="gate")
            for m in range(PACK):
                column = PACK * half + m
                nc.tensor.transpose(spread[:, m, :], weight_runs[:, column : column + 1].to_broadcast([P, P]), identity[:])
            nc.scalar.copy(router_runs[:, :, PACK * half : PACK * (half + 1)], spread[:].rearrange("p m q -> p q m"))

        tok = [held("tok%d" % a, [P, J], U32) for a in range(PASSES)]
        tok_rows = held("tok_rows", [P, J], U8)
        nc.vector.tensor_copy(tok_rows[:], tab_rows[:].indirect(offsets[:]))
        for q in range(QUADS):
            nc.sync.dma_start(
                tok_planes[32 * q : 32 * q + 4, :].bitcast(I32), tok_rows[96 + 8 * q : 96 + 8 * q + 8, :].bitcast(I32)
            )
        load_wg(1, early.tile([P, PACK, R], F32, name="wg_raw1", offset=0, align_bytes=64))
        load_tab(1, early.tile([P, T], I32, name="tab1", offset=4 * T, align_bytes=64))

        planes_by_slot = wu_planes[:].bitcast(I32).rearrange("p (a s g w) -> p a s g w", a=PASSES, s=PACK, w=2)
        for q in range(QUADS):
            nc.vector.tensor_copy(
                planes_by_slot[32 * q : 32 * q + 4],
                wu_rows[0:4, :, q, :].rearrange("p a (g s w) -> p a s g w", s=PACK, w=2),
            )
        wu = held("wu", [P, PASSES, 2 * R], U8)
        nc.scalar.copy(
            wu[:].bitcast(U32).rearrange("p a (s g w) -> p a s g w", s=PACK, w=4),
            wu_raw[:].bitcast(U32).rearrange("p a (g s w) -> p a s g w", s=PACK, w=4),
        )

        for start in (0, HALF):
            nc.vector.tensor_copy(
                tok[0][:, start : start + HALF], tab[0][:].bitcast(U32).indirect(listed(start, start + HALF))
            )

        pages.append(paged.tile([P, T], F32, name="page1", offset=0, align_bytes=64))
        nc.vector.memset(pages[1][:].bitcast(I32), 0)

        wg_codes = [held("wg_codes%d" % a, [P, R], U32) for a in range(PASSES)]
        wg_plane = [held("wg_plane%d" % a, [P, R], U8) for a in range(PASSES)]
        for a in range(PASSES):
            if a == 0:
                wg_bf = late.tile([P, PACK * R], BF16, name="wg_bf0", offset=WD_AT, align_bytes=64)
            else:
                wg_bf = held("wg_bf1", [P, PACK * R], BF16)
            dst = wg_bf[:].rearrange("p (s g u c i) -> p s g u i c", s=PACK, u=2, c=4, i=PACK)
            src = wg_raw[a][:].rearrange("p i (g s u c) -> p s g u i c", s=PACK, u=2, c=4)
            for s in range(PACK):
                if a == PASSES - 1 and s >= PACK // 2:
                    nc.vector.tensor_copy(dst[:, s], src[:, s])
                else:
                    nc.scalar.copy(dst[:, s], src[:, s])
            for s in range(0, PACK, 2):
                cols = slice(P * s, P * (s + 2))
                nc.vector.quantize_mx(
                    out=wg_codes[a][:, cols].bitcast(FP8X4),
                    scales=wg_plane[a][:, cols],
                    in_=wg_bf[:, K_PASS * s : K_PASS * (s + 2)],
                )

        load_gates(0, "wg_raw0")
        wd_raw = {}
        wd_rows = wd.rearrange("(g s q) n -> s g q n", s=PACK, q=8)

        def load_wd(u, tile):
            wd_raw[u] = tile
            for s in range(PACK):
                nc.sync.dma_start(tile[:, s, :], wd_rows[s, :, :, N // 2 * u : N // 2 * (u + 1)])

        load_wd(0, late.tile([P, PACK, N // 2], F32, name="wd_raw0", offset=WD_AT, align_bytes=64))
        gates[1] = early.tile([P, T], F32, name="gates1", offset=0, align_bytes=64)
        nc.sync.dma_start(gates[1][:], gT[P : 2 * P, :])

        ups = {}
        gas = {}
        acts = {}
        lifted = {}
        factors = []
        gated = {}
        h_codes = [held("h_codes%d" % u, [P, HALF], U32) for u in range(2)]
        h_plane = [
            late.tile([P, HALF], U8, name="h_plane0", offset=WD_AT - HALF + 64, align_bytes=64),
            held("h_plane1", [P, HALF], U8),
        ]
        y_half = {}
        y_half[0, 0] = late.tile([P, HALF], F32, name="y00", offset=8 * HALF - 64, align_bytes=64)
        y_half[1, 0] = held("y10", [P, HALF], F32)
        y_half[0, 1] = held("y01", [P, HALF], F32)
        y_half[1, 1] = held("y11", [P, HALF], F32)
        y_whole = {n: held("y%d" % n, [P, J], F32) for n in range(PAGES, N_TILES)}

        def y_part(n, u):
            if n < PAGES:
                return y_half[n, u][:]
            return y_whole[n][:, HALF * u : HALF * (u + 1)]

        def first_pass(acc, jt, a, weights, planes):
            for s in range(PACK):
                nc.tensor.matmul_mx(
                    out=acc[:, s, :],
                    lhsT=weights(s),
                    lhsT_scale=planes(s),
                    rhs=tok[a][:, P * jt : P * (jt + 1)].bitcast(FP8X4),
                    rhs_scale=tok_planes[:, J * a + P * jt : J * a + P * (jt + 1)],
                    start=(a == 0 and s == 0),
                    stop=(a == PASSES - 1 and s == PACK - 1),
                )

        def up_pass(jt, a):
            if a == 0:
                ups[jt] = psum.tile([P, PACK, P], F32, name="ub", tag="up")
            first_pass(
                ups[jt],
                jt,
                a,
                lambda s: wu[:, a, 2 * P * s : 2 * P * (s + 1)].bitcast(FP4X4),
                lambda s: wu_planes[:, R * a + P * s : R * a + P * (s + 1)],
            )

        def gate_pass(jt, a):
            if a == 0:
                gas[jt] = psum.tile([P, PACK, P], F32, name="ga", tag="gate")
            first_pass(
                gas[jt],
                jt,
                a,
                lambda s: wg_codes[a][:, P * s : P * (s + 1)].bitcast(FP8X4),
                lambda s: wg_plane[a][:, P * s : P * (s + 1)],
            )

        def finish_tile(jt):
            if jt >= BANKS:
                gate_pass(jt, 0)
            gate_pass(jt, 1)
            if jt < BANKS:
                acts[jt] = held("act%d" % jt, [P, P, PACK], F32)[:]
            else:
                acts[jt] = factors[0][:, 0, jt - BANKS]
            nc.scalar.activation(acts[jt], gas[jt][:].rearrange("p s j -> p j s"), GELU)
            if jt >= BANKS:
                up_pass(jt, 0)
            up_pass(jt, 1)
            if jt >= BANKS:
                lifted[jt] = factors[0][:, 1, jt - BANKS]
                nc.scalar.copy(lifted[jt], ups[jt][:].rearrange("p s j -> p j s"))

        def h_slot(tile, jt):
            place = jt % BANKS
            return tile[:, K_PASS * place : K_PASS * (place + 1)].rearrange("p (j s) -> p j s", s=PACK)

        def quantise_h(u, tile):
            nc.vector.quantize_mx(out=h_codes[u][:].bitcast(FP8X4), scales=h_plane[u][:], in_=tile[:])

        def gather_gates(n, tile):
            gated[n] = tile
            nc.vector.tensor_tensor(gated[n][:], gates[n][:].indirect(offsets[:]), router[:], MULT)

        wd_codes = held("wd_codes", [P, N], U32)
        wd_plane = [held("wd_plane0", [P, N // 2], U8)]
        wd_bf = [held("wd_bf%d" % u, [P, PACK * N // 2], BF16) for u in range(2)]

        def round_wd(u):
            dst = wd_bf[u][:].rearrange("p (m c s) -> p m s c", c=4, s=PACK)
            nc.scalar.copy(dst, wd_raw[u][:].rearrange("p s (m c) -> p m s c", c=4))

        def quantise_wd(u):
            cols = slice(2 * P * u, 2 * P * (u + 1))
            nc.vector.quantize_mx(
                out=wd_codes[:, cols].bitcast(FP8X4),
                scales=wd_plane[u][:],
                in_=wd_bf[u][:],
            )

        def second_stage(n, u):
            acc = psum.tile([P, HALF], F32, name="acc", tag="gate")
            nc.tensor.matmul_mx(
                out=acc[:],
                lhsT=wd_codes[:, P * n : P * (n + 1)].bitcast(FP8X4),
                lhsT_scale=wd_plane[n // 2][:, P * (n % 2) : P * (n % 2 + 1)],
                rhs=h_codes[u][:].bitcast(FP8X4),
                rhs_scale=h_plane[u][:],
                start=True,
                stop=True,
            )
            nc.scalar.copy(y_part(n, u), acc[:])

        def scatter(n, start, stop, values):
            nc.vector.tensor_tensor(
                pages[n % PAGES][:].indirect(listed(start, stop)), values, gated[n][:, start:stop], MULT
            )

        def store(n):
            nc.sync.dma_start(out[P * n : P * (n + 1), :], pages[n % PAGES][:])

        for jt in range(BANKS):
            up_pass(jt, 0)
        for jt in range(BANKS):
            gate_pass(jt, 0)
        for start, stop in ((0, 2 * P), (2 * P, HALF), (HALF, J)):
            nc.vector.tensor_copy(tok[1][:, start:stop], tab[1][:].bitcast(U32).indirect(listed(start, stop)))
        gates[2] = early.tile([P, T], F32, name="gates2", offset=4 * T, align_bytes=64)
        nc.sync.dma_start(gates[2][:], gT[2 * P : 3 * P, :])

        h_first = held("h_first", [P, BANKS * K_PASS], BF16)
        for jt in range(BANKS):
            finish_tile(jt)
            nc.vector.tensor_tensor(
                h_slot(h_first, jt), ups[jt][:].rearrange("p s j -> p j s"), acts[jt], MULT
            )
            if jt == 1:
                gather_gates(0, held("gated0", [P, J], F32))
        load_wd(1, held("wd_raw1", [P, PACK, N // 2], F32, after="act0"))
        load_gates(3, "act1")
        round_wd(0)
        quantise_wd(0)
        quantise_h(0, h_first)
        gather_gates(1, held("gated1", [P, J], F32, after="wd_bf0"))
        factors.append(late.tile([P, 2, BANKS, P, PACK], F32, name="factors", offset=FACTORS_AT, align_bytes=64))
        for jt in range(BANKS, J_TILES - 1):
            finish_tile(jt)
        for n in range(PAGES):
            second_stage(n, 0)
        finish_tile(J_TILES - 1)
        round_wd(1)

        ready0 = held("ready0", [P, HALF], F32)
        nc.vector.tensor_tensor(ready0[:], y_half[0, 0][:], gated[0][:, 0:HALF], MULT)
        ready1 = late.tile([P, HALF], F32, name="ready1", offset=12 * HALF - 128, align_bytes=64)
        nc.gpsimd.tensor_tensor(ready1[:], y_half[1, 0][:], gated[1][:, 0:HALF], MULT)
        h_second = late.tile([P, BANKS * K_PASS], BF16, name="h_second", offset=0, align_bytes=64)
        both = factors[0][:].rearrange("p f t j s -> p f (t j s)")
        nc.gpsimd.tensor_tensor(h_second[:], both[:, 1], both[:, 0], MULT)
        for n, ready in enumerate((ready0, ready1)):
            nc.vector.tensor_copy(pages[n][:].indirect(listed(0, HALF)), ready[:])

        quantise_h(1, h_second)
        wd_plane.append(late.tile([P, N // 2], U8, name="wd_plane1", offset=FACTORS_AT + HALF + 4 * J, align_bytes=64))
        quantise_wd(1)
        gather_gates(2, late.tile([P, J], F32, name="gated2", offset=FACTORS_AT + HALF, align_bytes=64))
        for n in range(PAGES):
            second_stage(n, 1)
        for n in range(PAGES, N_TILES):
            for u in range(2):
                second_stage(n, u)
        for n in range(PAGES):
            scatter(n, HALF, J, y_half[n, 1][:])
            store(n)
        gather_gates(3, held("gated3", [P, J], F32, after="y01"))
        scatter(2, 0, J, y_whole[2][:])
        store(2)
        last = N_TILES - 1
        scatter(last, 0, J, y_whole[last][:])
        for queue, cols in ((nc.sync, slice(0, T // 2)), (nc.scalar, slice(T // 2, T))):
            queue.dma_start(out[P * last : P * (last + 1), cols], pages[last % PAGES][:, cols])
